import numpy as np
import ml_dtypes


def mxq(x, axis, fmt="e4m3"):
    dtype, down = {"e4m3": (ml_dtypes.float8_e4m3fn, 7), "e5m2": (ml_dtypes.float8_e5m2, 14)}[fmt]
    v = np.moveaxis(np.asarray(x, np.float32).astype(ml_dtypes.bfloat16).astype(np.float64), axis, -1)
    blocks = v.reshape(v.shape[:-1] + (-1, 32))
    amax = np.abs(blocks).max(-1, keepdims=True)
    byte = np.maximum(np.where(amax > 0, np.frexp(amax)[1] - 1 + 127, 0) - down, 1)
    scale = np.exp2(byte - 127.0)
    codes = (blocks / scale).astype(np.float32).astype(dtype).astype(np.float64)
    return np.moveaxis((codes * scale).reshape(v.shape), -1, axis)


WIDE = False


def mx_kscale(k):
    if not WIDE:
        return np.ones(k)
    levels = np.array([10, -10, 5, -5, 0])
    if k % 512:
        return np.exp2(np.random.permutation(np.resize(levels, k // 32))).repeat(32)
    a = np.empty((k // 512, 16))
    for p in range(k // 512):
        a[p, :8] = np.random.permutation(np.resize(levels, 8))
        for g in range(8):
            far = levels[np.abs(levels - a[p, g]) >= 10]
            a[p, g + 8] = far[np.random.randint(len(far))]
    return np.exp2(a.ravel()).repeat(32)


def f64(x):
    return np.asarray(x).astype(np.float64)


def striped(idx):
    return np.tile(np.asarray(idx).reshape(-1, 16).T, (8, 1)).astype(np.uint16)


def unstriped(offs):
    return offs[:16].T.reshape(-1).astype(np.int64)


E2M1 = np.array([0.0, 0.5, 1.0, 1.5, 2.0, 3.0, 4.0, 6.0, -0.0, -0.5, -1.0, -1.5, -2.0, -3.0, -4.0, -6.0])


def pack_weight(w, fmt):
    k, n = w.shape
    w = f64(np.asarray(w, np.float32).astype(ml_dtypes.bfloat16)).reshape(k // 32, 32, n)
    amax = np.abs(w).max(1)
    if fmt == "e4m3":
        byte = np.frexp(amax)[1] - 1 + 127 - 7
    else:
        mant, ex = np.frexp(amax / 6.0)
        byte = np.where(mant > 0.5, ex, ex - 1) + 127
    byte = np.clip(np.where(amax > 0, byte, 1), 1, 254)
    scaled = (w * np.exp2(127.0 - byte)[:, None, :]).reshape(k, n).astype(np.float32)
    by_word = np.ascontiguousarray(scaled.reshape(k // 512, 128, 4, n).transpose(0, 1, 3, 2))
    if fmt == "e4m3":
        words = by_word.astype(ml_dtypes.float8_e4m3fn).view(np.uint8)
    else:
        c = by_word.astype(ml_dtypes.float4_e2m1fn).view(np.uint8) & 0xF
        words = (c[..., 0::2] | (c[..., 1::2] << 4)).reshape(k // 512, 128, 2 * n)
    return np.ascontiguousarray(words), np.ascontiguousarray(byte.astype(np.uint8).reshape(k // 512, 16, n))


def unpack_weight(words, scales, fmt):
    g, _, n = scales.shape
    words = np.ascontiguousarray(words).reshape(g, 128, n, -1)
    if fmt == "e4m3":
        vals = words.view(ml_dtypes.float8_e4m3fn).astype(np.float64)
    else:
        nib = np.empty((g, 128, n, 4), np.uint8)
        nib[..., 0::2] = words & 0xF
        nib[..., 1::2] = words >> 4
        vals = E2M1[nib]
    vals = vals * np.repeat(np.exp2(scales.astype(np.float64) - 127.0), 8, axis=1)[..., None]
    return vals.transpose(0, 1, 3, 2).reshape(g * 512, n)


def sigmoid(v):
    return 1.0 / (1.0 + np.exp(-v))


B, N, T, D, NQ = 1, 512, 2048, 512, 256


def setup_inputs():
    n = np.random.standard_normal
    idx = np.random.permutation(T)[:B * N]
    idx2 = np.random.permutation(1024)[:B * N]
    s = mx_kscale(D)[:, None]
    kp = pack_weight(n((D, T)) / s, "e4m3")
    cp = pack_weight(n((D, 1024)) / s, "e4m3")
    return {
        "uT": (n((B, D, NQ)) * s * (1.00 / np.sqrt(D))).astype(np.float32),
        "vT": (n((B, D, NQ)) * s * (1.00 / np.sqrt(D))).astype(np.float32),
        "k_words": kp[0],
        "k_scales": kp[1],
        "c_words": cp[0],
        "c_scales": cp[1],
        "kb": np.tile(n(2048), (128, 1)).astype(np.float32),
        "offs": striped(idx),
        "offs2": striped(idx2),
    }


def reference(uT, vT, k_words, k_scales, c_words, c_scales, kb, offs, offs2):
    idx = unstriped(offs)
    idx2 = unstriped(offs2)
    pick = lambda x, which: x[:, which].reshape(x.shape[0], B, -1).transpose(1, 0, 2)
    k = unpack_weight(k_words, k_scales, "e4m3")
    kg = pick(k, idx)
    c = unpack_weight(c_words, c_scales, "e4m3")
    cg = pick(c, idx2)
    uq = mxq(f64(uT), 1, "e4m3")
    vq = mxq(f64(vT), 1, "e4m3")
    a = (uq.transpose(0, 2, 1) @ kg) + (vq.transpose(0, 2, 1) @ cg)
    y = sigmoid(a / 4.0 + pick(f64(kb), idx)[:, :1, :])
    return y

@@ -1,0 +1,149 @@
+from contextlib import ExitStack
+
+import concourse.mybir as mybir
+from concourse.masks import make_identity
+
+F32 = mybir.dt.float32
+BF16 = mybir.dt.bfloat16
+I32 = mybir.dt.int32
+U32 = mybir.dt.uint32
+U16 = mybir.dt.uint16
+U8 = mybir.dt.uint8
+FP8X4 = mybir.dt.float8_e4m3fn_x4
+ACT = mybir.ActivationFunctionType
+ALU = mybir.AluOpType
+
+P = 128
+PACK = 4
+D = 512
+NQ = 256
+SLOTS = 512
+HALF = 256
+TOKENS = 2048
+DISTANCES = 1024
+
+FLOPS = 2 * 2 * D * NQ * SLOTS
+BYTES = 3219456
+
+
+def load_scale_rows(queue, window, scales):
+    rows = scales[0].bitcast(I32)
+    for quad in range(4):
+        queue.dma_start(out=window[32 * quad : 32 * quad + 4, :], in_=rows[4 * quad : 4 * quad + 4, :])
+
+
+def tile_attend_txlsig_topk_kernel(tc, uT, vT, k_words, k_scales, c_words, c_scales, kb, offs, offs2, out):
+    nc = tc.nc
+    with ExitStack() as ctx:
+        held = ctx.enter_context(tc.tile_pool(name="held", bufs=1))
+        psum = ctx.enter_context(tc.psum_pool(name="psum", bufs=1))
+
+        token_list = held.tile([P, SLOTS // 16], U16, name="token_list")
+        distance_list = held.tile([P, SLOTS // 16], U16, name="distance_list")
+        k_word_pool = held.tile([P, TOKENS], I32, name="k_word_pool", align_bytes=64)
+        c_word_pool = held.tile([P, DISTANCES], I32, name="c_word_pool", align_bytes=64)
+        k_scale_pool = held.tile([P, TOKENS // 4], I32, name="k_scale_pool", align_bytes=64)
+        c_scale_pool = held.tile([P, DISTANCES // 4], I32, name="c_scale_pool", align_bytes=64)
+        kb_pool = held.tile([P, TOKENS], F32, name="kb_pool", align_bytes=64)
+        u_raw = held.tile([P, PACK, NQ], F32, name="u_raw", align_bytes=64)
+        v_raw = held.tile([P, PACK, NQ], F32, name="v_raw", align_bytes=64)
+        identity = held.tile([P, P], F32, name="identity", align_bytes=64)
+        warm_in = held.tile([P, 8], F32, name="warm_in")
+        warm_out = held.tile([P, 8], F32, name="warm_out")
+
+        nc.gpsimd.memset(warm_in[:], 0.0)
+        nc.scalar.activation(out=warm_out[:], in_=warm_in[:], func=ACT.Sigmoid)
+        make_identity(nc, identity[:])
+
+        nc.vector.memset(c_scale_pool[:], 0)
+        nc.vector.memset(kb_pool[:], 0.0)
+        nc.vector.memset(k_scale_pool[:], 0)
+
+        nc.sync.dma_start(distance_list[:], offs2)
+        nc.sync.dma_start(out=c_word_pool[:], in_=c_words[0].rearrange("p n t -> p (n t)").bitcast(I32))
+        load_scale_rows(nc.sync, c_scale_pool, c_scales)
+        nc.sync.dma_start(token_list[:], offs)
+        nc.sync.dma_start(out=v_raw[:], in_=vT[0].rearrange("(p j) q -> p j q", j=PACK))
+        nc.sync.dma_start(out=u_raw[:], in_=uT[0].rearrange("(p j) q -> p j q", j=PACK))
+        nc.sync.dma_start(out=k_word_pool[:], in_=k_words[0].rearrange("p n t -> p (n t)").bitcast(I32))
+        nc.scalar.dma_start(out=kb_pool[0:1, :], in_=kb[0:1, :])
+        load_scale_rows(nc.scalar, k_scale_pool, k_scales)
+
+        c_codes = held.tile([P, SLOTS], U32, name="c_codes", align_bytes=64)
+        c_bytes = held.tile([P, SLOTS], U8, name="c_bytes", align_bytes=64)
+        k_codes = held.tile([P, SLOTS], U32, name="k_codes", align_bytes=64)
+        k_bytes = held.tile([P, SLOTS], U8, name="k_bytes", align_bytes=64)
+        kb_row = held.tile([P, SLOTS], F32, name="kb_row", align_bytes=64)
+        nc.vector.tensor_copy(c_codes[:], c_word_pool[:].bitcast(U32).indirect(distance_list[:]))
+        nc.vector.tensor_copy(c_bytes[:], c_scale_pool[:].bitcast(U8).indirect(distance_list[:]))
+        nc.vector.tensor_copy(kb_row[:], kb_pool[:].indirect(token_list[:]))
+        nc.vector.tensor_copy(k_bytes[:], k_scale_pool[:].bitcast(U8).indirect(token_list[:]))
+
+        quantised = {}
+        for name, raw in (("v", v_raw), ("u", u_raw)):
+            grouped = held.tile([P, NQ, PACK], BF16, name=name + "_grouped", align_bytes=64)
+            codes = held.tile([P, NQ], U32, name=name + "_codes", align_bytes=64)
+            scale_bytes = held.tile([P, NQ], U8, name=name + "_bytes", align_bytes=64)
+            nc.scalar.copy(out=grouped[:], in_=raw[:].rearrange("p j q -> p q j"))
+            nc.vector.quantize_mx(
+                out=codes[:].bitcast(FP8X4),
+                scales=scale_bytes[:],
+                in_=grouped[:].rearrange("p q j -> p (q j)"),
+            )
+            quantised[name] = (codes, scale_bytes)
+
+        turned = psum.tile([P, SLOTS // P, P], F32, name="turned")
+        for blk in range(SLOTS // P):
+            nc.tensor.transpose(turned[:, blk, :], kb_row[:, blk * P : (blk + 1) * P], identity[:])
+        kb_column = held.tile([P, SLOTS // P], F32, name="kb_column", align_bytes=64)
+        nc.scalar.copy(out=kb_column[:], in_=turned[:, :, 0])
+        bias = held.tile([P, SLOTS], F32, name="bias", align_bytes=64)
+        for half in range(2):
+            spread = psum.tile([P, HALF], F32, name="spread%d" % half)
+            for sub in range(HALF // P):
+                blk = half * (HALF // P) + sub
+                nc.tensor.transpose(
+                    spread[:, sub * P : (sub + 1) * P], kb_column[:, blk : blk + 1].to_broadcast([P, P]), identity[:]
+                )
+            nc.scalar.copy(out=bias[:, half * HALF : (half + 1) * HALF], in_=spread[:])
+
+        pieces = [(half, qt) for half in range(2) for qt in range(NQ // P)]
+        acc = {}
+        for half, qt in pieces:
+            acc[half, qt] = psum.tile([P, HALF], F32, name="acc%d%d" % (half, qt))
+            q_cols = slice(qt * P, (qt + 1) * P)
+            s_cols = slice(half * HALF, (half + 1) * HALF)
+            nc.tensor.matmul_mx(
+                out=acc[half, qt][:],
+                lhsT=quantised["v"][0][:, q_cols].bitcast(FP8X4),
+                lhsT_scale=quantised["v"][1][:, q_cols],
+                rhs=c_codes[:, s_cols].bitcast(FP8X4),
+                rhs_scale=c_bytes[:, s_cols],
+                start=True,
+                stop=False,
+            )
+
+        for half in range(2):
+            s_cols = slice(half * HALF, (half + 1) * HALF)
+            entries = token_list[:, half * (HALF // 16) : (half + 1) * (HALF // 16)]
+            nc.vector.tensor_copy(k_codes[:, s_cols], k_word_pool[:].bitcast(U32).indirect(entries))
+
+        for half, qt in pieces:
+            q_cols = slice(qt * P, (qt + 1) * P)
+            s_cols = slice(half * HALF, (half + 1) * HALF)
+            nc.tensor.matmul_mx(
+                out=acc[half, qt][:],
+                lhsT=quantised["u"][0][:, q_cols].bitcast(FP8X4),
+                lhsT_scale=quantised["u"][1][:, q_cols],
+                rhs=k_codes[:, s_cols].bitcast(FP8X4),
+                rhs_scale=k_bytes[:, s_cols],
+                start=False,
+                stop=True,
+            )
+            logit = held.tile([P, HALF], F32, name="logit%d%d" % (half, qt), align_bytes=64)
+            nc.vector.scalar_tensor_tensor(
+                out=logit[:], in0=acc[half, qt][:], scalar=0.25, in1=bias[:, s_cols], op0=ALU.mult, op1=ALU.add
+            )
+            weight = held.tile([P, HALF], F32, name="weight%d%d" % (half, qt), align_bytes=64)
+            nc.scalar.activation(out=weight[:], in_=logit[:], func=ACT.Sigmoid)
+            nc.sync.dma_start(out=out[0, q_cols, s_cols], in_=weight[:])

@@ -26,9 +26,9 @@ FLOPS = 2 * 2 * D * NQ * SLOTS
 BYTES = 3219456
 
 
-def load_scale_rows(queue, window, scales):
+def load_scale_rows(queues, window, scales):
     rows = scales[0].bitcast(I32)
-    for quad in range(4):
+    for quad, queue in enumerate(queues):
         queue.dma_start(out=window[32 * quad : 32 * quad + 4, :], in_=rows[4 * quad : 4 * quad + 4, :])
 
 
@@ -42,47 +42,47 @@ def tile_attend_txlsig_topk_kernel(tc, uT, vT, k_words, k_scales, c_words, c_sca
         distance_list = held.tile([P, SLOTS // 16], U16, name="distance_list")
         k_word_pool = held.tile([P, TOKENS], I32, name="k_word_pool", align_bytes=64)
         c_word_pool = held.tile([P, DISTANCES], I32, name="c_word_pool", align_bytes=64)
-        k_scale_pool = held.tile([P, TOKENS // 4], I32, name="k_scale_pool", align_bytes=64)
+        k_scale_pool = held.tile([P, TOKENS // 4], I32, name="k_scale_pool", tag="u_codes", align_bytes=64)
         c_scale_pool = held.tile([P, DISTANCES // 4], I32, name="c_scale_pool", align_bytes=64)
-        kb_pool = held.tile([P, TOKENS], F32, name="kb_pool", align_bytes=64)
-        u_raw = held.tile([P, PACK, NQ], F32, name="u_raw", align_bytes=64)
+        kb_pool = held.tile([P, TOKENS], F32, name="kb_pool", tag="v_codes", align_bytes=64)
+        u_raw = held.tile([P, PACK, NQ], F32, name="u_raw", tag="kb_column", align_bytes=64)
         v_raw = held.tile([P, PACK, NQ], F32, name="v_raw", align_bytes=64)
         identity = held.tile([P, P], F32, name="identity", align_bytes=64)
         warm_in = held.tile([P, 8], F32, name="warm_in")
         warm_out = held.tile([P, 8], F32, name="warm_out")
 
-        nc.gpsimd.memset(warm_in[:], 0.0)
-        nc.scalar.activation(out=warm_out[:], in_=warm_in[:], func=ACT.Sigmoid)
         make_identity(nc, identity[:])
 
         nc.vector.memset(c_scale_pool[:], 0)
+        nc.vector.memset(warm_in[:], 0.0)
         nc.vector.memset(kb_pool[:], 0.0)
         nc.vector.memset(k_scale_pool[:], 0)
 
         nc.sync.dma_start(distance_list[:], offs2)
+        load_scale_rows([nc.scalar, nc.scalar, nc.sync, nc.sync], c_scale_pool, c_scales)
         nc.sync.dma_start(out=c_word_pool[:], in_=c_words[0].rearrange("p n t -> p (n t)").bitcast(I32))
-        load_scale_rows(nc.sync, c_scale_pool, c_scales)
         nc.sync.dma_start(token_list[:], offs)
         nc.sync.dma_start(out=v_raw[:], in_=vT[0].rearrange("(p j) q -> p j q", j=PACK))
+        nc.sync.dma_start(out=kb_pool[0:1, :], in_=kb[0:1, :])
         nc.sync.dma_start(out=u_raw[:], in_=uT[0].rearrange("(p j) q -> p j q", j=PACK))
+        load_scale_rows([nc.sync] * 4, k_scale_pool, k_scales)
         nc.sync.dma_start(out=k_word_pool[:], in_=k_words[0].rearrange("p n t -> p (n t)").bitcast(I32))
-        nc.scalar.dma_start(out=kb_pool[0:1, :], in_=kb[0:1, :])
-        load_scale_rows(nc.scalar, k_scale_pool, k_scales)
+        nc.scalar.activation(out=warm_out[:], in_=warm_in[:], func=ACT.Sigmoid)
 
         c_codes = held.tile([P, SLOTS], U32, name="c_codes", align_bytes=64)
         c_bytes = held.tile([P, SLOTS], U8, name="c_bytes", align_bytes=64)
         k_codes = held.tile([P, SLOTS], U32, name="k_codes", align_bytes=64)
         k_bytes = held.tile([P, SLOTS], U8, name="k_bytes", align_bytes=64)
         kb_row = held.tile([P, SLOTS], F32, name="kb_row", align_bytes=64)
-        nc.vector.tensor_copy(c_codes[:], c_word_pool[:].bitcast(U32).indirect(distance_list[:]))
         nc.vector.tensor_copy(c_bytes[:], c_scale_pool[:].bitcast(U8).indirect(distance_list[:]))
+        nc.vector.tensor_copy(c_codes[:], c_word_pool[:].bitcast(U32).indirect(distance_list[:]))
         nc.vector.tensor_copy(kb_row[:], kb_pool[:].indirect(token_list[:]))
         nc.vector.tensor_copy(k_bytes[:], k_scale_pool[:].bitcast(U8).indirect(token_list[:]))
 
         quantised = {}
         for name, raw in (("v", v_raw), ("u", u_raw)):
             grouped = held.tile([P, NQ, PACK], BF16, name=name + "_grouped", align_bytes=64)
-            codes = held.tile([P, NQ], U32, name=name + "_codes", align_bytes=64)
+            codes = held.tile([P, NQ], U32, name=name + "_codes", tag=name + "_codes", align_bytes=64)
             scale_bytes = held.tile([P, NQ], U8, name=name + "_bytes", align_bytes=64)
             nc.scalar.copy(out=grouped[:], in_=raw[:].rearrange("p j q -> p q j"))
             nc.vector.quantize_mx(
@@ -95,7 +95,7 @@ def tile_attend_txlsig_topk_kernel(tc, uT, vT, k_words, k_scales, c_words, c_sca
         turned = psum.tile([P, SLOTS // P, P], F32, name="turned")
         for blk in range(SLOTS // P):
             nc.tensor.transpose(turned[:, blk, :], kb_row[:, blk * P : (blk + 1) * P], identity[:])
-        kb_column = held.tile([P, SLOTS // P], F32, name="kb_column", align_bytes=64)
+        kb_column = held.tile([P, SLOTS // P], F32, name="kb_column", tag="kb_column", align_bytes=64)
         nc.scalar.copy(out=kb_column[:], in_=turned[:, :, 0])
         bias = held.tile([P, SLOTS], F32, name="bias", align_bytes=64)
         for half in range(2):

@@ -21,15 +21,26 @@ SLOTS = 512
 HALF = 256
 TOKENS = 2048
 DISTANCES = 1024
+KB_SPLIT = 1024
+LAST_WIDTH = 128
 
 FLOPS = 2 * 2 * D * NQ * SLOTS
 BYTES = 3219456
 
 
-def load_scale_rows(queues, window, scales):
+def load_scale_rows(queue, window, scales, quads):
     rows = scales[0].bitcast(I32)
-    for quad, queue in enumerate(queues):
+    for quad in quads:
         queue.dma_start(out=window[32 * quad : 32 * quad + 4, :], in_=rows[4 * quad : 4 * quad + 4, :])
+
+
+def fill_scale_rows(queue, window, scales, quads):
+    rows = scales[0].bitcast(I32)
+    for quad in quads:
+        four = rows[4 * quad : 4 * quad + 4, :]
+        queue.dma_start(
+            out=window[32 * quad : 32 * quad + 32, :], in_=four.unsqueeze(0).to_broadcast([8, 4, four.shape[1]])
+        )
 
 
 def tile_attend_txlsig_topk_kernel(tc, uT, vT, k_words, k_scales, c_words, c_scales, kb, offs, offs2, out):
@@ -42,30 +53,32 @@ def tile_attend_txlsig_topk_kernel(tc, uT, vT, k_words, k_scales, c_words, c_sca
         distance_list = held.tile([P, SLOTS // 16], U16, name="distance_list")
         k_word_pool = held.tile([P, TOKENS], I32, name="k_word_pool", align_bytes=64)
         c_word_pool = held.tile([P, DISTANCES], I32, name="c_word_pool", align_bytes=64)
-        k_scale_pool = held.tile([P, TOKENS // 4], I32, name="k_scale_pool", tag="u_codes", align_bytes=64)
+        k_scale_pool = held.tile([P, TOKENS // 4], I32, name="k_scale_pool", align_bytes=64)
         c_scale_pool = held.tile([P, DISTANCES // 4], I32, name="c_scale_pool", align_bytes=64)
-        kb_pool = held.tile([P, TOKENS], F32, name="kb_pool", tag="v_codes", align_bytes=64)
+        kb_pool = held.tile([P, TOKENS], F32, name="kb_pool", align_bytes=64)
         u_raw = held.tile([P, PACK, NQ], F32, name="u_raw", tag="kb_column", align_bytes=64)
         v_raw = held.tile([P, PACK, NQ], F32, name="v_raw", align_bytes=64)
         identity = held.tile([P, P], F32, name="identity", align_bytes=64)
         warm_in = held.tile([P, 8], F32, name="warm_in")
         warm_out = held.tile([P, 8], F32, name="warm_out")
 
+        nc.gpsimd.memset(kb_pool[:, KB_SPLIT:], 0.0)
         make_identity(nc, identity[:])
 
-        nc.vector.memset(c_scale_pool[:], 0)
         nc.vector.memset(warm_in[:], 0.0)
-        nc.vector.memset(kb_pool[:], 0.0)
+        nc.vector.memset(kb_pool[:, :KB_SPLIT], 0.0)
         nc.vector.memset(k_scale_pool[:], 0)
 
         nc.sync.dma_start(distance_list[:], offs2)
-        load_scale_rows([nc.scalar, nc.scalar, nc.sync, nc.sync], c_scale_pool, c_scales)
+        fill_scale_rows(nc.scalar, c_scale_pool, c_scales, [0, 1])
+        fill_scale_rows(nc.sync, c_scale_pool, c_scales, [2, 3])
         nc.sync.dma_start(out=c_word_pool[:], in_=c_words[0].rearrange("p n t -> p (n t)").bitcast(I32))
-        nc.sync.dma_start(token_list[:], offs)
-        nc.sync.dma_start(out=v_raw[:], in_=vT[0].rearrange("(p j) q -> p j q", j=PACK))
         nc.sync.dma_start(out=kb_pool[0:1, :], in_=kb[0:1, :])
+        nc.sync.dma_start(out=v_raw[:], in_=vT[0].rearrange("(p j) q -> p j q", j=PACK))
+        nc.sync.dma_start(token_list[:], offs)
+        load_scale_rows(nc.sync, k_scale_pool, k_scales, [0, 1, 2])
         nc.sync.dma_start(out=u_raw[:], in_=uT[0].rearrange("(p j) q -> p j q", j=PACK))
-        load_scale_rows([nc.sync] * 4, k_scale_pool, k_scales)
+        load_scale_rows(nc.sync, k_scale_pool, k_scales, [3])
         nc.sync.dma_start(out=k_word_pool[:], in_=k_words[0].rearrange("p n t -> p (n t)").bitcast(I32))
         nc.scalar.activation(out=warm_out[:], in_=warm_in[:], func=ACT.Sigmoid)
 
@@ -111,39 +124,48 @@ def tile_attend_txlsig_topk_kernel(tc, uT, vT, k_words, k_scales, c_words, c_sca
         acc = {}
         for half, qt in pieces:
             acc[half, qt] = psum.tile([P, HALF], F32, name="acc%d%d" % (half, qt))
+
+        def product(piece, queries, codes, scale_bytes, first):
+            half, qt = piece
             q_cols = slice(qt * P, (qt + 1) * P)
             s_cols = slice(half * HALF, (half + 1) * HALF)
             nc.tensor.matmul_mx(
-                out=acc[half, qt][:],
-                lhsT=quantised["v"][0][:, q_cols].bitcast(FP8X4),
-                lhsT_scale=quantised["v"][1][:, q_cols],
-                rhs=c_codes[:, s_cols].bitcast(FP8X4),
-                rhs_scale=c_bytes[:, s_cols],
-                start=True,
-                stop=False,
+                out=acc[piece][:],
+                lhsT=quantised[queries][0][:, q_cols].bitcast(FP8X4),
+                lhsT_scale=quantised[queries][1][:, q_cols],
+                rhs=codes[:, s_cols].bitcast(FP8X4),
+                rhs_scale=scale_bytes[:, s_cols],
+                start=first,
+                stop=not first,
             )
+
+        for piece in pieces[:-1]:
+            product(piece, "v", c_codes, c_bytes, True)
 
         for half in range(2):
             s_cols = slice(half * HALF, (half + 1) * HALF)
             entries = token_list[:, half * (HALF // 16) : (half + 1) * (HALF // 16)]
             nc.vector.tensor_copy(k_codes[:, s_cols], k_word_pool[:].bitcast(U32).indirect(entries))
 
-        for half, qt in pieces:
-            q_cols = slice(qt * P, (qt + 1) * P)
-            s_cols = slice(half * HALF, (half + 1) * HALF)
-            nc.tensor.matmul_mx(
-                out=acc[half, qt][:],
-                lhsT=quantised["u"][0][:, q_cols].bitcast(FP8X4),
-                lhsT_scale=quantised["u"][1][:, q_cols],
-                rhs=k_codes[:, s_cols].bitcast(FP8X4),
-                rhs_scale=k_bytes[:, s_cols],
-                start=False,
-                stop=True,
-            )
-            logit = held.tile([P, HALF], F32, name="logit%d%d" % (half, qt), align_bytes=64)
-            nc.vector.scalar_tensor_tensor(
-                out=logit[:], in0=acc[half, qt][:], scalar=0.25, in1=bias[:, s_cols], op0=ALU.mult, op1=ALU.add
-            )
-            weight = held.tile([P, HALF], F32, name="weight%d%d" % (half, qt), align_bytes=64)
-            nc.scalar.activation(out=weight[:], in_=logit[:], func=ACT.Sigmoid)
-            nc.sync.dma_start(out=out[0, q_cols, s_cols], in_=weight[:])
+        for piece in pieces:
+            half, qt = piece
+            last = piece == pieces[-1]
+            product(piece, "u", k_codes, k_bytes, last)
+            if last:
+                product(piece, "v", c_codes, c_bytes, False)
+            width = LAST_WIDTH if last else HALF
+            for col in range(0, HALF, width):
+                s_cols = slice(half * HALF + col, half * HALF + col + width)
+                label = "%d%d_%d" % (half, qt, col)
+                logit = held.tile([P, width], F32, name="logit" + label, align_bytes=64)
+                nc.vector.scalar_tensor_tensor(
+                    out=logit[:],
+                    in0=acc[piece][:, col : col + width],
+                    scalar=0.25,
+                    in1=bias[:, s_cols],
+                    op0=ALU.mult,
+                    op1=ALU.add,
+                )
+                weight = held.tile([P, width], F32, name="weight" + label, align_bytes=64)
+                nc.scalar.activation(out=weight[:], in_=logit[:], func=ACT.Sigmoid)
+                nc.sync.dma_start(out=out[0, qt * P : (qt + 1) * P, s_cols], in_=weight[:])

@@ -22,6 +22,7 @@ HALF = 256
 TOKENS = 2048
 DISTANCES = 1024
 KB_SPLIT = 1024
+KB_PARTITION = 80
 LAST_WIDTH = 128
 
 FLOPS = 2 * 2 * D * NQ * SLOTS
@@ -30,8 +31,8 @@ BYTES = 3219456
 
 def load_scale_rows(queue, window, scales, quads):
     rows = scales[0].bitcast(I32)
-    for quad in quads:
-        queue.dma_start(out=window[32 * quad : 32 * quad + 4, :], in_=rows[4 * quad : 4 * quad + 4, :])
+    for row in quads:
+        queue.dma_start(out=window[row:P:32, :], in_=rows[row:16:4, :])
 
 
 def fill_scale_rows(queue, window, scales, quads):
@@ -73,7 +74,7 @@ def tile_attend_txlsig_topk_kernel(tc, uT, vT, k_words, k_scales, c_words, c_sca
         fill_scale_rows(nc.scalar, c_scale_pool, c_scales, [0, 1])
         fill_scale_rows(nc.sync, c_scale_pool, c_scales, [2, 3])
         nc.sync.dma_start(out=c_word_pool[:], in_=c_words[0].rearrange("p n t -> p (n t)").bitcast(I32))
-        nc.sync.dma_start(out=kb_pool[0:1, :], in_=kb[0:1, :])
+        nc.sync.dma_start(out=kb_pool[KB_PARTITION : KB_PARTITION + 1, :], in_=kb[0:1, :])
         nc.sync.dma_start(out=v_raw[:], in_=vT[0].rearrange("(p j) q -> p j q", j=PACK))
         nc.sync.dma_start(token_list[:], offs)
         load_scale_rows(nc.sync, k_scale_pool, k_scales, [0, 1, 2])
@@ -109,7 +110,7 @@ def tile_attend_txlsig_topk_kernel(tc, uT, vT, k_words, k_scales, c_words, c_sca
         for blk in range(SLOTS // P):
             nc.tensor.transpose(turned[:, blk, :], kb_row[:, blk * P : (blk + 1) * P], identity[:])
         kb_column = held.tile([P, SLOTS // P], F32, name="kb_column", tag="kb_column", align_bytes=64)
-        nc.scalar.copy(out=kb_column[:], in_=turned[:, :, 0])
+        nc.scalar.copy(out=kb_column[:], in_=turned[:, :, KB_PARTITION])
         bias = held.tile([P, SLOTS], F32, name="bias", align_bytes=64)
         for half in range(2):
             spread = psum.tile([P, HALF], F32, name="spread%d" % half)

@@ -21,7 +21,6 @@ SLOTS = 512
 HALF = 256
 TOKENS = 2048
 DISTANCES = 1024
-KB_SPLIT = 1024
 KB_PARTITION = 80
 LAST_WIDTH = 128
 
@@ -63,12 +62,12 @@ def tile_attend_txlsig_topk_kernel(tc, uT, vT, k_words, k_scales, c_words, c_sca
         warm_in = held.tile([P, 8], F32, name="warm_in")
         warm_out = held.tile([P, 8], F32, name="warm_out")
 
-        nc.gpsimd.memset(kb_pool[:, KB_SPLIT:], 0.0)
-        make_identity(nc, identity[:])
 
         nc.vector.memset(warm_in[:], 0.0)
-        nc.vector.memset(kb_pool[:, :KB_SPLIT], 0.0)
+        nc.vector.memset(kb_pool[:], 0.0)
         nc.vector.memset(k_scale_pool[:], 0)
+        nc.vector.memset(identity[:], 0.0)
+        make_identity(nc, identity[:], nomemset=True)
 
         nc.sync.dma_start(distance_list[:], offs2)
         fill_scale_rows(nc.scalar, c_scale_pool, c_scales, [0, 1])
@@ -98,7 +97,10 @@ def tile_attend_txlsig_topk_kernel(tc, uT, vT, k_words, k_scales, c_words, c_sca
             grouped = held.tile([P, NQ, PACK], BF16, name=name + "_grouped", align_bytes=64)
             codes = held.tile([P, NQ], U32, name=name + "_codes", tag=name + "_codes", align_bytes=64)
             scale_bytes = held.tile([P, NQ], U8, name=name + "_bytes", align_bytes=64)
-            nc.scalar.copy(out=grouped[:], in_=raw[:].rearrange("p j q -> p q j"))
+            nc.scalar.copy(
+                out=grouped[:].rearrange("p (c i) j -> p c j i", i=4),
+                in_=raw[:].rearrange("p j (c i) -> p c j i", i=4),
+            )
             nc.vector.quantize_mx(
                 out=codes[:].bitcast(FP8X4),
                 scales=scale_bytes[:],

@@ -21,26 +21,18 @@ SLOTS = 512
 HALF = 256
 TOKENS = 2048
 DISTANCES = 1024
-KB_PARTITION = 80
+KB_PARTITION = 127
+SCALE_PARTITION = 112
 LAST_WIDTH = 128
 
 FLOPS = 2 * 2 * D * NQ * SLOTS
 BYTES = 3219456
 
 
-def load_scale_rows(queue, window, scales, quads):
-    rows = scales[0].bitcast(I32)
-    for row in quads:
-        queue.dma_start(out=window[row:P:32, :], in_=rows[row:16:4, :])
-
-
-def fill_scale_rows(queue, window, scales, quads):
-    rows = scales[0].bitcast(I32)
+def place_scale_rows(queue, plane, gathered, quads):
     for quad in quads:
-        four = rows[4 * quad : 4 * quad + 4, :]
-        queue.dma_start(
-            out=window[32 * quad : 32 * quad + 32, :], in_=four.unsqueeze(0).to_broadcast([8, 4, four.shape[1]])
-        )
+        first = SCALE_PARTITION + 4 * quad
+        queue.dma_start(out=plane[32 * quad : 32 * quad + 4, :], in_=gathered[:].bitcast(I32)[first : first + 4, :])
 
 
 def tile_attend_txlsig_topk_kernel(tc, uT, vT, k_words, k_scales, c_words, c_scales, kb, offs, offs2, out):
@@ -52,51 +44,54 @@ def tile_attend_txlsig_topk_kernel(tc, uT, vT, k_words, k_scales, c_words, c_sca
         token_list = held.tile([P, SLOTS // 16], U16, name="token_list")
         distance_list = held.tile([P, SLOTS // 16], U16, name="distance_list")
         k_word_pool = held.tile([P, TOKENS], I32, name="k_word_pool", align_bytes=64)
-        c_word_pool = held.tile([P, DISTANCES], I32, name="c_word_pool", align_bytes=64)
+        c_word_pool = held.tile([P, DISTANCES], I32, name="c_word_pool", tag="u_codes", align_bytes=64)
         k_scale_pool = held.tile([P, TOKENS // 4], I32, name="k_scale_pool", align_bytes=64)
         c_scale_pool = held.tile([P, DISTANCES // 4], I32, name="c_scale_pool", align_bytes=64)
-        kb_pool = held.tile([P, TOKENS], F32, name="kb_pool", align_bytes=64)
-        u_raw = held.tile([P, PACK, NQ], F32, name="u_raw", tag="kb_column", align_bytes=64)
+        kb_pool = held.tile([P, TOKENS], F32, name="kb_pool", tag="k_listed", align_bytes=64)
+        u_raw = held.tile([P, PACK, NQ], F32, name="u_raw", align_bytes=64)
         v_raw = held.tile([P, PACK, NQ], F32, name="v_raw", align_bytes=64)
         identity = held.tile([P, P], F32, name="identity", align_bytes=64)
         warm_in = held.tile([P, 8], F32, name="warm_in")
         warm_out = held.tile([P, 8], F32, name="warm_out")
 
 
-        nc.vector.memset(warm_in[:], 0.0)
-        nc.vector.memset(kb_pool[:], 0.0)
-        nc.vector.memset(k_scale_pool[:], 0)
+        nc.vector.memset(c_scale_pool[0:SCALE_PARTITION, :], 0)
+        nc.vector.memset(k_scale_pool[0:SCALE_PARTITION, :], 0)
+        nc.vector.memset(kb_pool[0:KB_PARTITION, :], 0.0)
         nc.vector.memset(identity[:], 0.0)
+        nc.vector.memset(warm_in[:], 0.0)
         make_identity(nc, identity[:], nomemset=True)
 
         nc.sync.dma_start(distance_list[:], offs2)
-        fill_scale_rows(nc.scalar, c_scale_pool, c_scales, [0, 1])
-        fill_scale_rows(nc.sync, c_scale_pool, c_scales, [2, 3])
+        nc.scalar.dma_start(out=c_scale_pool[SCALE_PARTITION:P, :], in_=c_scales[0].bitcast(I32))
         nc.sync.dma_start(out=c_word_pool[:], in_=c_words[0].rearrange("p n t -> p (n t)").bitcast(I32))
-        nc.sync.dma_start(out=kb_pool[KB_PARTITION : KB_PARTITION + 1, :], in_=kb[0:1, :])
-        nc.sync.dma_start(out=v_raw[:], in_=vT[0].rearrange("(p j) q -> p j q", j=PACK))
+        nc.scalar.dma_start(out=kb_pool[KB_PARTITION:P, :], in_=kb[0:1, :])
+        nc.scalar.dma_start(out=k_scale_pool[SCALE_PARTITION:P, :], in_=k_scales[0].bitcast(I32))
         nc.sync.dma_start(token_list[:], offs)
-        load_scale_rows(nc.sync, k_scale_pool, k_scales, [0, 1, 2])
+        nc.sync.dma_start(out=v_raw[:], in_=vT[0].rearrange("(p j) q -> p j q", j=PACK))
         nc.sync.dma_start(out=u_raw[:], in_=uT[0].rearrange("(p j) q -> p j q", j=PACK))
-        load_scale_rows(nc.sync, k_scale_pool, k_scales, [3])
-        nc.sync.dma_start(out=k_word_pool[:], in_=k_words[0].rearrange("p n t -> p (n t)").bitcast(I32))
         nc.scalar.activation(out=warm_out[:], in_=warm_in[:], func=ACT.Sigmoid)
 
-        c_codes = held.tile([P, SLOTS], U32, name="c_codes", align_bytes=64)
-        c_bytes = held.tile([P, SLOTS], U8, name="c_bytes", align_bytes=64)
         k_codes = held.tile([P, SLOTS], U32, name="k_codes", align_bytes=64)
-        k_bytes = held.tile([P, SLOTS], U8, name="k_bytes", align_bytes=64)
-        kb_row = held.tile([P, SLOTS], F32, name="kb_row", align_bytes=64)
-        nc.vector.tensor_copy(c_bytes[:], c_scale_pool[:].bitcast(U8).indirect(distance_list[:]))
-        nc.vector.tensor_copy(c_codes[:], c_word_pool[:].bitcast(U32).indirect(distance_list[:]))
+        c_listed = held.tile([P, SLOTS], U8, name="c_listed", align_bytes=64)
+        c_plane = held.tile([P, SLOTS // 4], I32, name="c_plane", align_bytes=64)
+        k_plane = held.tile([P, SLOTS // 4], I32, name="k_plane", align_bytes=64)
+        kb_row = held.tile([P, SLOTS], F32, name="kb_row", tag="c_codes", align_bytes=64)
+        nc.vector.tensor_copy(c_listed[:], c_scale_pool[:].bitcast(U8).indirect(distance_list[:]))
+        place_scale_rows(nc.scalar, c_plane, c_listed, [0, 1])
+        place_scale_rows(nc.sync, c_plane, c_listed, [2, 3])
+        nc.sync.dma_start(out=k_word_pool[:], in_=k_words[0].rearrange("p n t -> p (n t)").bitcast(I32))
         nc.vector.tensor_copy(kb_row[:], kb_pool[:].indirect(token_list[:]))
-        nc.vector.tensor_copy(k_bytes[:], k_scale_pool[:].bitcast(U8).indirect(token_list[:]))
+        k_listed = held.tile([P, SLOTS], U8, name="k_listed", tag="k_listed", align_bytes=64)
+        nc.vector.tensor_copy(k_listed[:], k_scale_pool[:].bitcast(U8).indirect(token_list[:]))
+        place_scale_rows(nc.sync, k_plane, k_listed, range(4))
+        c_bytes = c_plane[:].bitcast(U8)
+        k_bytes = k_plane[:].bitcast(U8)
 
-        quantised = {}
-        for name, raw in (("v", v_raw), ("u", u_raw)):
-            grouped = held.tile([P, NQ, PACK], BF16, name=name + "_grouped", align_bytes=64)
-            codes = held.tile([P, NQ], U32, name=name + "_codes", tag=name + "_codes", align_bytes=64)
-            scale_bytes = held.tile([P, NQ], U8, name=name + "_bytes", align_bytes=64)
+        def quantise(label, raw):
+            grouped = held.tile([P, NQ, PACK], BF16, name=label + "_grouped", align_bytes=64)
+            codes = held.tile([P, NQ], U32, name=label + "_codes", tag=label + "_codes", align_bytes=64)
+            scale_bytes = held.tile([P, NQ], U8, name=label + "_bytes", align_bytes=64)
             nc.scalar.copy(
                 out=grouped[:].rearrange("p (c i) j -> p c j i", i=4),
                 in_=raw[:].rearrange("p j (c i) -> p c j i", i=4),
@@ -106,29 +101,32 @@ def tile_attend_txlsig_topk_kernel(tc, uT, vT, k_words, k_scales, c_words, c_sca
                 scales=scale_bytes[:],
                 in_=grouped[:].rearrange("p q j -> p (q j)"),
             )
-            quantised[name] = (codes, scale_bytes)
+            return codes, scale_bytes
+
+        quantised = {"v": quantise("v", v_raw)}
 
         turned = psum.tile([P, SLOTS // P, P], F32, name="turned")
         for blk in range(SLOTS // P):
             nc.tensor.transpose(turned[:, blk, :], kb_row[:, blk * P : (blk + 1) * P], identity[:])
-        kb_column = held.tile([P, SLOTS // P], F32, name="kb_column", tag="kb_column", align_bytes=64)
+        c_codes = held.tile([P, SLOTS], U32, name="c_codes", tag="c_codes", align_bytes=64)
+        nc.vector.tensor_copy(c_codes[:], c_word_pool[:].bitcast(U32).indirect(distance_list[:]))
+        kb_column = held.tile([P, SLOTS // P], F32, name="kb_column", align_bytes=64)
         nc.scalar.copy(out=kb_column[:], in_=turned[:, :, KB_PARTITION])
+        quantised["u"] = quantise("u", u_raw)
         bias = held.tile([P, SLOTS], F32, name="bias", align_bytes=64)
-        for half in range(2):
-            spread = psum.tile([P, HALF], F32, name="spread%d" % half)
-            for sub in range(HALF // P):
-                blk = half * (HALF // P) + sub
-                nc.tensor.transpose(
-                    spread[:, sub * P : (sub + 1) * P], kb_column[:, blk : blk + 1].to_broadcast([P, P]), identity[:]
-                )
-            nc.scalar.copy(out=bias[:, half * HALF : (half + 1) * HALF], in_=spread[:])
+        spread = psum.tile([P, SLOTS], F32, name="spread")
+        for blk in range(SLOTS // P):
+            nc.tensor.transpose(
+                spread[:, blk * P : (blk + 1) * P], kb_column[:, blk : blk + 1].to_broadcast([P, P]), identity[:]
+            )
+        nc.scalar.copy(out=bias[:], in_=spread[:])
 
         pieces = [(half, qt) for half in range(2) for qt in range(NQ // P)]
         acc = {}
-        for half, qt in pieces:
-            acc[half, qt] = psum.tile([P, HALF], F32, name="acc%d%d" % (half, qt))
+        for piece in pieces:
+            acc[piece] = psum.tile([P, HALF], F32, name="acc%d_%d" % piece)
 
-        def product(piece, queries, codes, scale_bytes, first):
+        def product(piece, queries, codes, scale_bytes, first_pass):
             half, qt = piece
             q_cols = slice(qt * P, (qt + 1) * P)
             s_cols = slice(half * HALF, (half + 1) * HALF)
@@ -138,28 +136,26 @@ def tile_attend_txlsig_topk_kernel(tc, uT, vT, k_words, k_scales, c_words, c_sca
                 lhsT_scale=quantised[queries][1][:, q_cols],
                 rhs=codes[:, s_cols].bitcast(FP8X4),
                 rhs_scale=scale_bytes[:, s_cols],
-                start=first,
-                stop=not first,
+                start=first_pass,
+                stop=not first_pass,
             )
 
-        for piece in pieces[:-1]:
+        for piece in pieces:
             product(piece, "v", c_codes, c_bytes, True)
 
         for half in range(2):
-            s_cols = slice(half * HALF, (half + 1) * HALF)
             entries = token_list[:, half * (HALF // 16) : (half + 1) * (HALF // 16)]
-            nc.vector.tensor_copy(k_codes[:, s_cols], k_word_pool[:].bitcast(U32).indirect(entries))
+            nc.vector.tensor_copy(
+                k_codes[:, half * HALF : (half + 1) * HALF], k_word_pool[:].bitcast(U32).indirect(entries)
+            )
 
         for piece in pieces:
             half, qt = piece
-            last = piece == pieces[-1]
-            product(piece, "u", k_codes, k_bytes, last)
-            if last:
-                product(piece, "v", c_codes, c_bytes, False)
-            width = LAST_WIDTH if last else HALF
+            product(piece, "u", k_codes, k_bytes, False)
+            width = LAST_WIDTH if piece == pieces[-1] else HALF
             for col in range(0, HALF, width):
                 s_cols = slice(half * HALF + col, half * HALF + col + width)
-                label = "%d%d_%d" % (half, qt, col)
+                label = "%d_%d_%d" % (qt, half, col)
                 logit = held.tile([P, width], F32, name="logit" + label, align_bytes=64)
                 nc.vector.scalar_tensor_tensor(
                     out=logit[:],

@@ -24,6 +24,7 @@ DISTANCES = 1024
 KB_PARTITION = 127
 SCALE_PARTITION = 112
 LAST_WIDTH = 128
+EARLY_TOKENS = 512
 
 FLOPS = 2 * 2 * D * NQ * SLOTS
 BYTES = 3219456
@@ -39,15 +40,16 @@ def tile_attend_txlsig_topk_kernel(tc, uT, vT, k_words, k_scales, c_words, c_sca
     nc = tc.nc
     with ExitStack() as ctx:
         held = ctx.enter_context(tc.tile_pool(name="held", bufs=1))
+        shared = ctx.enter_context(tc.tile_pool(name="shared", bufs=1))
         psum = ctx.enter_context(tc.psum_pool(name="psum", bufs=1))
 
         token_list = held.tile([P, SLOTS // 16], U16, name="token_list")
         distance_list = held.tile([P, SLOTS // 16], U16, name="distance_list")
         k_word_pool = held.tile([P, TOKENS], I32, name="k_word_pool", align_bytes=64)
-        c_word_pool = held.tile([P, DISTANCES], I32, name="c_word_pool", tag="u_codes", align_bytes=64)
-        k_scale_pool = held.tile([P, TOKENS // 4], I32, name="k_scale_pool", align_bytes=64)
-        c_scale_pool = held.tile([P, DISTANCES // 4], I32, name="c_scale_pool", align_bytes=64)
-        kb_pool = held.tile([P, TOKENS], F32, name="kb_pool", tag="k_listed", align_bytes=64)
+        c_word_pool = held.tile([P, DISTANCES], I32, name="c_word_pool", align_bytes=64)
+        k_scale_pool = held.tile([P, TOKENS // 4 + 1], I32, name="k_scale_pool", align_bytes=64)
+        c_scale_pool = held.tile([P, DISTANCES // 4 + 1], I32, name="c_scale_pool", align_bytes=64)
+        kb_pool = held.tile([P, TOKENS], F32, name="kb_pool", align_bytes=64)
         u_raw = held.tile([P, PACK, NQ], F32, name="u_raw", align_bytes=64)
         v_raw = held.tile([P, PACK, NQ], F32, name="v_raw", align_bytes=64)
         identity = held.tile([P, P], F32, name="identity", align_bytes=64)
@@ -57,41 +59,41 @@ def tile_attend_txlsig_topk_kernel(tc, uT, vT, k_words, k_scales, c_words, c_sca
 
         nc.vector.memset(c_scale_pool[0:SCALE_PARTITION, :], 0)
         nc.vector.memset(k_scale_pool[0:SCALE_PARTITION, :], 0)
-        nc.vector.memset(kb_pool[0:KB_PARTITION, :], 0.0)
-        nc.vector.memset(identity[:], 0.0)
-        nc.vector.memset(warm_in[:], 0.0)
-        make_identity(nc, identity[:], nomemset=True)
+        nc.gpsimd.memset(kb_pool[0:KB_PARTITION, :], 0.0)
+        nc.vector.memset(warm_in[:, 0:7], 0.0)
+        make_identity(nc, identity[:])
 
         nc.sync.dma_start(distance_list[:], offs2)
-        nc.scalar.dma_start(out=c_scale_pool[SCALE_PARTITION:P, :], in_=c_scales[0].bitcast(I32))
+        nc.scalar.dma_start(out=c_scale_pool[SCALE_PARTITION:P, 0 : DISTANCES // 4], in_=c_scales[0].bitcast(I32))
         nc.sync.dma_start(out=c_word_pool[:], in_=c_words[0].rearrange("p n t -> p (n t)").bitcast(I32))
         nc.scalar.dma_start(out=kb_pool[KB_PARTITION:P, :], in_=kb[0:1, :])
-        nc.scalar.dma_start(out=k_scale_pool[SCALE_PARTITION:P, :], in_=k_scales[0].bitcast(I32))
+        nc.scalar.dma_start(out=k_scale_pool[SCALE_PARTITION:P, 0 : TOKENS // 4], in_=k_scales[0].bitcast(I32))
         nc.sync.dma_start(token_list[:], offs)
         nc.sync.dma_start(out=v_raw[:], in_=vT[0].rearrange("(p j) q -> p j q", j=PACK))
         nc.sync.dma_start(out=u_raw[:], in_=uT[0].rearrange("(p j) q -> p j q", j=PACK))
-        nc.scalar.activation(out=warm_out[:], in_=warm_in[:], func=ACT.Sigmoid)
+        key_words = k_words[0].rearrange("p n t -> p (n t)").bitcast(I32)
+        nc.sync.dma_start(out=k_word_pool[:, 0:EARLY_TOKENS], in_=key_words[:, 0:EARLY_TOKENS])
+        nc.scalar.activation(out=warm_out[:, 0:7], in_=warm_in[:, 0:7], func=ACT.Sigmoid)
 
-        k_codes = held.tile([P, SLOTS], U32, name="k_codes", align_bytes=64)
         c_listed = held.tile([P, SLOTS], U8, name="c_listed", align_bytes=64)
         c_plane = held.tile([P, SLOTS // 4], I32, name="c_plane", align_bytes=64)
         k_plane = held.tile([P, SLOTS // 4], I32, name="k_plane", align_bytes=64)
-        kb_row = held.tile([P, SLOTS], F32, name="kb_row", tag="c_codes", align_bytes=64)
-        nc.vector.tensor_copy(c_listed[:], c_scale_pool[:].bitcast(U8).indirect(distance_list[:]))
+        kb_row = shared.tile([P, SLOTS], F32, name="kb_row", align_bytes=64, offset=1024)
+        nc.vector.tensor_copy(c_listed[:], c_scale_pool[:, 0 : DISTANCES // 4].bitcast(U8).indirect(distance_list[:]))
         place_scale_rows(nc.scalar, c_plane, c_listed, [0, 1])
         place_scale_rows(nc.sync, c_plane, c_listed, [2, 3])
-        nc.sync.dma_start(out=k_word_pool[:], in_=k_words[0].rearrange("p n t -> p (n t)").bitcast(I32))
+        nc.sync.dma_start(out=k_word_pool[:, EARLY_TOKENS:], in_=key_words[:, EARLY_TOKENS:])
         nc.vector.tensor_copy(kb_row[:], kb_pool[:].indirect(token_list[:]))
-        k_listed = held.tile([P, SLOTS], U8, name="k_listed", tag="k_listed", align_bytes=64)
-        nc.vector.tensor_copy(k_listed[:], k_scale_pool[:].bitcast(U8).indirect(token_list[:]))
+        k_listed = held.tile([P, SLOTS], U8, name="k_listed", align_bytes=64)
+        nc.vector.tensor_copy(k_listed[:], k_scale_pool[:, 0 : TOKENS // 4].bitcast(U8).indirect(token_list[:]))
         place_scale_rows(nc.sync, k_plane, k_listed, range(4))
         c_bytes = c_plane[:].bitcast(U8)
         k_bytes = k_plane[:].bitcast(U8)
 
-        def quantise(label, raw):
+        def quantise(label, raw, offset):
             grouped = held.tile([P, NQ, PACK], BF16, name=label + "_grouped", align_bytes=64)
-            codes = held.tile([P, NQ], U32, name=label + "_codes", tag=label + "_codes", align_bytes=64)
-            scale_bytes = held.tile([P, NQ], U8, name=label + "_bytes", align_bytes=64)
+            codes = held.tile([P, NQ], U32, name=label + "_codes", align_bytes=64)
+            scale_bytes = shared.tile([P, NQ], U8, name=label + "_bytes", align_bytes=64, offset=offset)
             nc.scalar.copy(
                 out=grouped[:].rearrange("p (c i) j -> p c j i", i=4),
                 in_=raw[:].rearrange("p j (c i) -> p c j i", i=4),
@@ -103,16 +105,20 @@ def tile_attend_txlsig_topk_kernel(tc, uT, vT, k_words, k_scales, c_words, c_sca
             )
             return codes, scale_bytes
 
-        quantised = {"v": quantise("v", v_raw)}
 
+        quantised = {"v": quantise("v", v_raw, 4608)}
         turned = psum.tile([P, SLOTS // P, P], F32, name="turned")
         for blk in range(SLOTS // P):
             nc.tensor.transpose(turned[:, blk, :], kb_row[:, blk * P : (blk + 1) * P], identity[:])
-        c_codes = held.tile([P, SLOTS], U32, name="c_codes", tag="c_codes", align_bytes=64)
-        nc.vector.tensor_copy(c_codes[:], c_word_pool[:].bitcast(U32).indirect(distance_list[:]))
         kb_column = held.tile([P, SLOTS // P], F32, name="kb_column", align_bytes=64)
-        nc.scalar.copy(out=kb_column[:], in_=turned[:, :, KB_PARTITION])
-        quantised["u"] = quantise("u", u_raw)
+        nc.vector.tensor_copy(out=kb_column[:], in_=turned[:, :, KB_PARTITION])
+        c_codes = shared.tile([P, SLOTS], U32, name="c_codes", align_bytes=64, offset=0)
+        for half in range(2):
+            entries = distance_list[:, half * (HALF // 16) : (half + 1) * (HALF // 16)]
+            nc.vector.tensor_copy(
+                c_codes[:, half * HALF : (half + 1) * HALF], c_word_pool[:].bitcast(U32).indirect(entries)
+            )
+        quantised["u"] = quantise("u", u_raw, 2304)
         bias = held.tile([P, SLOTS], F32, name="bias", align_bytes=64)
         spread = psum.tile([P, SLOTS], F32, name="spread")
         for blk in range(SLOTS // P):
@@ -143,6 +149,7 @@ def tile_attend_txlsig_topk_kernel(tc, uT, vT, k_words, k_scales, c_words, c_sca
         for piece in pieces:
             product(piece, "v", c_codes, c_bytes, True)
 
+        k_codes = shared.tile([P, SLOTS], U32, name="k_codes", align_bytes=64, offset=2560)
         for half in range(2):
             entries = token_list[:, half * (HALF // 16) : (half + 1) * (HALF // 16)]
             nc.vector.tensor_copy(

@@ -22,17 +22,19 @@ HALF = 256
 TOKENS = 2048
 DISTANCES = 1024
 KB_PARTITION = 127
-SCALE_PARTITION = 112
+C_SCALE_PARTITION = 112
+K_SCALE_PARTITION = 48
 LAST_WIDTH = 128
+KB_SPLIT = 1536
 EARLY_TOKENS = 512
 
 FLOPS = 2 * 2 * D * NQ * SLOTS
 BYTES = 3219456
 
 
-def place_scale_rows(queue, plane, gathered, quads):
+def place_scale_rows(queue, plane, gathered, top, quads):
     for quad in quads:
-        first = SCALE_PARTITION + 4 * quad
+        first = top + 4 * quad
         queue.dma_start(out=plane[32 * quad : 32 * quad + 4, :], in_=gathered[:].bitcast(I32)[first : first + 4, :])
 
 
@@ -49,7 +51,7 @@ def tile_attend_txlsig_topk_kernel(tc, uT, vT, k_words, k_scales, c_words, c_sca
         c_word_pool = held.tile([P, DISTANCES], I32, name="c_word_pool", align_bytes=64)
         k_scale_pool = held.tile([P, TOKENS // 4 + 1], I32, name="k_scale_pool", align_bytes=64)
         c_scale_pool = held.tile([P, DISTANCES // 4 + 1], I32, name="c_scale_pool", align_bytes=64)
-        kb_pool = held.tile([P, TOKENS], F32, name="kb_pool", align_bytes=64)
+        kb_pool = held.tile([P, TOKENS + 1], F32, name="kb_pool", align_bytes=64)
         u_raw = held.tile([P, PACK, NQ], F32, name="u_raw", align_bytes=64)
         v_raw = held.tile([P, PACK, NQ], F32, name="v_raw", align_bytes=64)
         identity = held.tile([P, P], F32, name="identity", align_bytes=64)
@@ -57,17 +59,19 @@ def tile_attend_txlsig_topk_kernel(tc, uT, vT, k_words, k_scales, c_words, c_sca
         warm_out = held.tile([P, 8], F32, name="warm_out")
 
 
-        nc.vector.memset(c_scale_pool[0:SCALE_PARTITION, :], 0)
-        nc.vector.memset(k_scale_pool[0:SCALE_PARTITION, :], 0)
-        nc.gpsimd.memset(kb_pool[0:KB_PARTITION, :], 0.0)
-        nc.vector.memset(warm_in[:, 0:7], 0.0)
+        nc.vector.memset(c_scale_pool[0:C_SCALE_PARTITION, :], 0)
+        nc.vector.memset(k_scale_pool[0:K_SCALE_PARTITION, :], 0)
+        nc.vector.memset(k_scale_pool[64:P, :], 0)
         make_identity(nc, identity[:])
+        nc.gpsimd.memset(kb_pool[0:KB_PARTITION, 0:KB_SPLIT], 0.0)
+        nc.vector.memset(kb_pool[0:KB_PARTITION, KB_SPLIT:], 0.0)
+        nc.vector.memset(warm_in[:, 0:7], 0.0)
 
         nc.sync.dma_start(distance_list[:], offs2)
-        nc.scalar.dma_start(out=c_scale_pool[SCALE_PARTITION:P, 0 : DISTANCES // 4], in_=c_scales[0].bitcast(I32))
+        nc.scalar.dma_start(out=c_scale_pool[C_SCALE_PARTITION:P, 0 : DISTANCES // 4], in_=c_scales[0].bitcast(I32))
         nc.sync.dma_start(out=c_word_pool[:], in_=c_words[0].rearrange("p n t -> p (n t)").bitcast(I32))
-        nc.scalar.dma_start(out=kb_pool[KB_PARTITION:P, :], in_=kb[0:1, :])
-        nc.scalar.dma_start(out=k_scale_pool[SCALE_PARTITION:P, 0 : TOKENS // 4], in_=k_scales[0].bitcast(I32))
+        nc.scalar.dma_start(out=kb_pool[KB_PARTITION:P, 0:TOKENS], in_=kb[0:1, :])
+        nc.scalar.dma_start(out=k_scale_pool[K_SCALE_PARTITION:64, 0 : TOKENS // 4], in_=k_scales[0].bitcast(I32))
         nc.sync.dma_start(token_list[:], offs)
         nc.sync.dma_start(out=v_raw[:], in_=vT[0].rearrange("(p j) q -> p j q", j=PACK))
         nc.sync.dma_start(out=u_raw[:], in_=uT[0].rearrange("(p j) q -> p j q", j=PACK))
@@ -80,13 +84,13 @@ def tile_attend_txlsig_topk_kernel(tc, uT, vT, k_words, k_scales, c_words, c_sca
         k_plane = held.tile([P, SLOTS // 4], I32, name="k_plane", align_bytes=64)
         kb_row = shared.tile([P, SLOTS], F32, name="kb_row", align_bytes=64, offset=1024)
         nc.vector.tensor_copy(c_listed[:], c_scale_pool[:, 0 : DISTANCES // 4].bitcast(U8).indirect(distance_list[:]))
-        place_scale_rows(nc.scalar, c_plane, c_listed, [0, 1])
-        place_scale_rows(nc.sync, c_plane, c_listed, [2, 3])
+        place_scale_rows(nc.scalar, c_plane, c_listed, C_SCALE_PARTITION, [0, 1])
+        place_scale_rows(nc.sync, c_plane, c_listed, C_SCALE_PARTITION, [2, 3])
         nc.sync.dma_start(out=k_word_pool[:, EARLY_TOKENS:], in_=key_words[:, EARLY_TOKENS:])
-        nc.vector.tensor_copy(kb_row[:], kb_pool[:].indirect(token_list[:]))
+        nc.vector.tensor_copy(kb_row[:], kb_pool[:, 0:TOKENS].indirect(token_list[:]))
         k_listed = held.tile([P, SLOTS], U8, name="k_listed", align_bytes=64)
         nc.vector.tensor_copy(k_listed[:], k_scale_pool[:, 0 : TOKENS // 4].bitcast(U8).indirect(token_list[:]))
-        place_scale_rows(nc.sync, k_plane, k_listed, range(4))
+        place_scale_rows(nc.sync, k_plane, k_listed, K_SCALE_PARTITION, range(4))
         c_bytes = c_plane[:].bitcast(U8)
         k_bytes = k_plane[:].bitcast(U8)
 

@@ -23,10 +23,9 @@ TOKENS = 2048
 DISTANCES = 1024
 KB_PARTITION = 127
 C_SCALE_PARTITION = 112
-K_SCALE_PARTITION = 48
+K_SCALE_PARTITION = 112
 LAST_WIDTH = 128
-KB_SPLIT = 1536
-EARLY_TOKENS = 512
+EARLY_TOKENS = 768
 
 FLOPS = 2 * 2 * D * NQ * SLOTS
 BYTES = 3219456
@@ -51,53 +50,47 @@ def tile_attend_txlsig_topk_kernel(tc, uT, vT, k_words, k_scales, c_words, c_sca
         c_word_pool = held.tile([P, DISTANCES], I32, name="c_word_pool", align_bytes=64)
         k_scale_pool = held.tile([P, TOKENS // 4 + 1], I32, name="k_scale_pool", align_bytes=64)
         c_scale_pool = held.tile([P, DISTANCES // 4 + 1], I32, name="c_scale_pool", align_bytes=64)
-        kb_pool = held.tile([P, TOKENS + 1], F32, name="kb_pool", align_bytes=64)
-        u_raw = held.tile([P, PACK, NQ], F32, name="u_raw", align_bytes=64)
+        kb_pool = held.tile([P, TOKENS], F32, name="kb_pool", align_bytes=64)
+        u_raw = held.tile([P, PACK, NQ], F32, name="u_raw", tag="k_codes", align_bytes=64)
         v_raw = held.tile([P, PACK, NQ], F32, name="v_raw", align_bytes=64)
         identity = held.tile([P, P], F32, name="identity", align_bytes=64)
-        warm_in = held.tile([P, 8], F32, name="warm_in")
-        warm_out = held.tile([P, 8], F32, name="warm_out")
 
 
         nc.vector.memset(c_scale_pool[0:C_SCALE_PARTITION, :], 0)
         nc.vector.memset(k_scale_pool[0:K_SCALE_PARTITION, :], 0)
-        nc.vector.memset(k_scale_pool[64:P, :], 0)
         make_identity(nc, identity[:])
-        nc.gpsimd.memset(kb_pool[0:KB_PARTITION, 0:KB_SPLIT], 0.0)
-        nc.vector.memset(kb_pool[0:KB_PARTITION, KB_SPLIT:], 0.0)
-        nc.vector.memset(warm_in[:, 0:7], 0.0)
+        nc.gpsimd.memset(kb_pool[0:KB_PARTITION, :], 0.0)
 
         nc.sync.dma_start(distance_list[:], offs2)
         nc.scalar.dma_start(out=c_scale_pool[C_SCALE_PARTITION:P, 0 : DISTANCES // 4], in_=c_scales[0].bitcast(I32))
         nc.sync.dma_start(out=c_word_pool[:], in_=c_words[0].rearrange("p n t -> p (n t)").bitcast(I32))
-        nc.scalar.dma_start(out=kb_pool[KB_PARTITION:P, 0:TOKENS], in_=kb[0:1, :])
-        nc.scalar.dma_start(out=k_scale_pool[K_SCALE_PARTITION:64, 0 : TOKENS // 4], in_=k_scales[0].bitcast(I32))
+        nc.scalar.dma_start(out=kb_pool[KB_PARTITION:P, :], in_=kb[0:1, :])
+        nc.scalar.dma_start(out=k_scale_pool[K_SCALE_PARTITION:P, 0 : TOKENS // 4], in_=k_scales[0].bitcast(I32))
         nc.sync.dma_start(token_list[:], offs)
         nc.sync.dma_start(out=v_raw[:], in_=vT[0].rearrange("(p j) q -> p j q", j=PACK))
         nc.sync.dma_start(out=u_raw[:], in_=uT[0].rearrange("(p j) q -> p j q", j=PACK))
         key_words = k_words[0].rearrange("p n t -> p (n t)").bitcast(I32)
         nc.sync.dma_start(out=k_word_pool[:, 0:EARLY_TOKENS], in_=key_words[:, 0:EARLY_TOKENS])
-        nc.scalar.activation(out=warm_out[:, 0:7], in_=warm_in[:, 0:7], func=ACT.Sigmoid)
 
         c_listed = held.tile([P, SLOTS], U8, name="c_listed", align_bytes=64)
         c_plane = held.tile([P, SLOTS // 4], I32, name="c_plane", align_bytes=64)
         k_plane = held.tile([P, SLOTS // 4], I32, name="k_plane", align_bytes=64)
         kb_row = shared.tile([P, SLOTS], F32, name="kb_row", align_bytes=64, offset=1024)
         nc.vector.tensor_copy(c_listed[:], c_scale_pool[:, 0 : DISTANCES // 4].bitcast(U8).indirect(distance_list[:]))
-        place_scale_rows(nc.scalar, c_plane, c_listed, C_SCALE_PARTITION, [0, 1])
-        place_scale_rows(nc.sync, c_plane, c_listed, C_SCALE_PARTITION, [2, 3])
+        place_scale_rows(nc.sync, c_plane, c_listed, C_SCALE_PARTITION, range(4))
         nc.sync.dma_start(out=k_word_pool[:, EARLY_TOKENS:], in_=key_words[:, EARLY_TOKENS:])
-        nc.vector.tensor_copy(kb_row[:], kb_pool[:, 0:TOKENS].indirect(token_list[:]))
+        for half in range(2):
+            entries = token_list[:, half * (HALF // 16) : (half + 1) * (HALF // 16)]
+            nc.vector.tensor_copy(kb_row[:, half * HALF : (half + 1) * HALF], kb_pool[:].indirect(entries))
         k_listed = held.tile([P, SLOTS], U8, name="k_listed", align_bytes=64)
         nc.vector.tensor_copy(k_listed[:], k_scale_pool[:, 0 : TOKENS // 4].bitcast(U8).indirect(token_list[:]))
         place_scale_rows(nc.sync, k_plane, k_listed, K_SCALE_PARTITION, range(4))
         c_bytes = c_plane[:].bitcast(U8)
         k_bytes = k_plane[:].bitcast(U8)
 
-        def quantise(label, raw, offset):
-            grouped = held.tile([P, NQ, PACK], BF16, name=label + "_grouped", align_bytes=64)
+        def quantise(label, raw, grouped):
             codes = held.tile([P, NQ], U32, name=label + "_codes", align_bytes=64)
-            scale_bytes = shared.tile([P, NQ], U8, name=label + "_bytes", align_bytes=64, offset=offset)
+            scale_bytes = held.tile([P, NQ], U8, name=label + "_bytes", align_bytes=64)
             nc.scalar.copy(
                 out=grouped[:].rearrange("p (c i) j -> p c j i", i=4),
                 in_=raw[:].rearrange("p j (c i) -> p c j i", i=4),
@@ -110,19 +103,21 @@ def tile_attend_txlsig_topk_kernel(tc, uT, vT, k_words, k_scales, c_words, c_sca
             return codes, scale_bytes
 
 
-        quantised = {"v": quantise("v", v_raw, 4608)}
+        v_grouped = held.tile([P, NQ, PACK], BF16, name="v_grouped", align_bytes=64)
+        quantised = {"v": quantise("v", v_raw, v_grouped)}
         turned = psum.tile([P, SLOTS // P, P], F32, name="turned")
         for blk in range(SLOTS // P):
             nc.tensor.transpose(turned[:, blk, :], kb_row[:, blk * P : (blk + 1) * P], identity[:])
         kb_column = held.tile([P, SLOTS // P], F32, name="kb_column", align_bytes=64)
-        nc.vector.tensor_copy(out=kb_column[:], in_=turned[:, :, KB_PARTITION])
+        nc.scalar.copy(out=kb_column[:], in_=turned[:, :, KB_PARTITION])
         c_codes = shared.tile([P, SLOTS], U32, name="c_codes", align_bytes=64, offset=0)
         for half in range(2):
             entries = distance_list[:, half * (HALF // 16) : (half + 1) * (HALF // 16)]
             nc.vector.tensor_copy(
                 c_codes[:, half * HALF : (half + 1) * HALF], c_word_pool[:].bitcast(U32).indirect(entries)
             )
-        quantised["u"] = quantise("u", u_raw, 2304)
+        u_grouped = shared.tile([P, NQ, PACK], BF16, name="u_grouped", align_bytes=64, offset=2048)
+        quantised["u"] = quantise("u", u_raw, u_grouped)
         bias = held.tile([P, SLOTS], F32, name="bias", align_bytes=64)
         spread = psum.tile([P, SLOTS], F32, name="spread")
         for blk in range(SLOTS // P):
@@ -153,7 +148,7 @@ def tile_attend_txlsig_topk_kernel(tc, uT, vT, k_words, k_scales, c_words, c_sca
         for piece in pieces:
             product(piece, "v", c_codes, c_bytes, True)
 
-        k_codes = shared.tile([P, SLOTS], U32, name="k_codes", align_bytes=64, offset=2560)
+        k_codes = held.tile([P, SLOTS], U32, name="k_codes", tag="k_codes", align_bytes=64)
         for half in range(2):
             entries = token_list[:, half * (HALF // 16) : (half + 1) * (HALF // 16)]
             nc.vector.tensor_copy(

@@ -25,7 +25,7 @@ KB_PARTITION = 127
 C_SCALE_PARTITION = 112
 K_SCALE_PARTITION = 112
 LAST_WIDTH = 128
-EARLY_TOKENS = 768
+EARLY_TOKENS = 1024
 
 FLOPS = 2 * 2 * D * NQ * SLOTS
 BYTES = 3219456

@@ -22,19 +22,11 @@ HALF = 256
 TOKENS = 2048
 DISTANCES = 1024
 KB_PARTITION = 127
-C_SCALE_PARTITION = 112
-K_SCALE_PARTITION = 112
+SCALE_PARTITION = 112
 LAST_WIDTH = 128
-EARLY_TOKENS = 1024
 
 FLOPS = 2 * 2 * D * NQ * SLOTS
 BYTES = 3219456
-
-
-def place_scale_rows(queue, plane, gathered, top, quads):
-    for quad in quads:
-        first = top + 4 * quad
-        queue.dma_start(out=plane[32 * quad : 32 * quad + 4, :], in_=gathered[:].bitcast(I32)[first : first + 4, :])
 
 
 def tile_attend_txlsig_topk_kernel(tc, uT, vT, k_words, k_scales, c_words, c_scales, kb, offs, offs2, out):
@@ -50,74 +42,72 @@ def tile_attend_txlsig_topk_kernel(tc, uT, vT, k_words, k_scales, c_words, c_sca
         c_word_pool = held.tile([P, DISTANCES], I32, name="c_word_pool", align_bytes=64)
         k_scale_pool = held.tile([P, TOKENS // 4 + 1], I32, name="k_scale_pool", align_bytes=64)
         c_scale_pool = held.tile([P, DISTANCES // 4 + 1], I32, name="c_scale_pool", align_bytes=64)
-        kb_pool = held.tile([P, TOKENS], F32, name="kb_pool", align_bytes=64)
-        u_raw = held.tile([P, PACK, NQ], F32, name="u_raw", tag="k_codes", align_bytes=64)
+        kb_pool = shared.tile([P, TOKENS], F32, name="kb_pool", align_bytes=64, offset=6400)
         v_raw = held.tile([P, PACK, NQ], F32, name="v_raw", align_bytes=64)
         identity = held.tile([P, P], F32, name="identity", align_bytes=64)
 
-
-        nc.vector.memset(c_scale_pool[0:C_SCALE_PARTITION, :], 0)
-        nc.vector.memset(k_scale_pool[0:K_SCALE_PARTITION, :], 0)
-        make_identity(nc, identity[:])
+        warm_in = held.tile([P, 1], F32, name="warm_in", align_bytes=64)
+        warm_out = held.tile([P, 1], F32, name="warm_out", align_bytes=64)
+        nc.gpsimd.memset(warm_in[:], 0.0)
+        nc.vector.memset(c_scale_pool[:], 0)
+        nc.vector.memset(k_scale_pool[0:SCALE_PARTITION, :], 0)
         nc.gpsimd.memset(kb_pool[0:KB_PARTITION, :], 0.0)
+        make_identity(nc, identity[:])
 
-        nc.sync.dma_start(distance_list[:], offs2)
-        nc.scalar.dma_start(out=c_scale_pool[C_SCALE_PARTITION:P, 0 : DISTANCES // 4], in_=c_scales[0].bitcast(I32))
-        nc.sync.dma_start(out=c_word_pool[:], in_=c_words[0].rearrange("p n t -> p (n t)").bitcast(I32))
-        nc.scalar.dma_start(out=kb_pool[KB_PARTITION:P, :], in_=kb[0:1, :])
-        nc.scalar.dma_start(out=k_scale_pool[K_SCALE_PARTITION:P, 0 : TOKENS // 4], in_=k_scales[0].bitcast(I32))
         nc.sync.dma_start(token_list[:], offs)
+        nc.scalar.dma_start(out=kb_pool[KB_PARTITION:P, :], in_=kb[0:1, :])
+        nc.sync.dma_start(out=k_scale_pool[SCALE_PARTITION:P, 0 : TOKENS // 4], in_=k_scales[0].bitcast(I32))
+        nc.sync.dma_start(out=c_word_pool[:], in_=c_words[0].rearrange("p n t -> p (n t)").bitcast(I32))
+        nc.scalar.activation(out=warm_out[:], in_=warm_in[:], func=ACT.Sigmoid)
+        nc.sync.dma_start(distance_list[:], offs2)
         nc.sync.dma_start(out=v_raw[:], in_=vT[0].rearrange("(p j) q -> p j q", j=PACK))
-        nc.sync.dma_start(out=u_raw[:], in_=uT[0].rearrange("(p j) q -> p j q", j=PACK))
-        key_words = k_words[0].rearrange("p n t -> p (n t)").bitcast(I32)
-        nc.sync.dma_start(out=k_word_pool[:, 0:EARLY_TOKENS], in_=key_words[:, 0:EARLY_TOKENS])
-
-        c_listed = held.tile([P, SLOTS], U8, name="c_listed", align_bytes=64)
-        c_plane = held.tile([P, SLOTS // 4], I32, name="c_plane", align_bytes=64)
-        k_plane = held.tile([P, SLOTS // 4], I32, name="k_plane", align_bytes=64)
-        kb_row = shared.tile([P, SLOTS], F32, name="kb_row", align_bytes=64, offset=1024)
-        nc.vector.tensor_copy(c_listed[:], c_scale_pool[:, 0 : DISTANCES // 4].bitcast(U8).indirect(distance_list[:]))
-        place_scale_rows(nc.sync, c_plane, c_listed, C_SCALE_PARTITION, range(4))
-        nc.sync.dma_start(out=k_word_pool[:, EARLY_TOKENS:], in_=key_words[:, EARLY_TOKENS:])
-        for half in range(2):
-            entries = token_list[:, half * (HALF // 16) : (half + 1) * (HALF // 16)]
-            nc.vector.tensor_copy(kb_row[:, half * HALF : (half + 1) * HALF], kb_pool[:].indirect(entries))
-        k_listed = held.tile([P, SLOTS], U8, name="k_listed", align_bytes=64)
-        nc.vector.tensor_copy(k_listed[:], k_scale_pool[:, 0 : TOKENS // 4].bitcast(U8).indirect(token_list[:]))
-        place_scale_rows(nc.sync, k_plane, k_listed, K_SCALE_PARTITION, range(4))
-        c_bytes = c_plane[:].bitcast(U8)
-        k_bytes = k_plane[:].bitcast(U8)
-
-        def quantise(label, raw, grouped):
-            codes = held.tile([P, NQ], U32, name=label + "_codes", align_bytes=64)
-            scale_bytes = held.tile([P, NQ], U8, name=label + "_bytes", align_bytes=64)
-            nc.scalar.copy(
-                out=grouped[:].rearrange("p (c i) j -> p c j i", i=4),
-                in_=raw[:].rearrange("p j (c i) -> p c j i", i=4),
+        for row in range(4):
+            nc.sync.dma_start(
+                out=c_scale_pool[row:P:32, 0 : DISTANCES // 4], in_=c_scales[0].bitcast(I32)[row:16:4, :]
             )
-            nc.vector.quantize_mx(
-                out=codes[:].bitcast(FP8X4),
-                scales=scale_bytes[:],
-                in_=grouped[:].rearrange("p q j -> p (q j)"),
-            )
-            return codes, scale_bytes
+        nc.sync.dma_start(out=k_word_pool[:], in_=k_words[0].rearrange("p n t -> p (n t)").bitcast(I32))
 
+        u_rows = uT[0].rearrange("(p j) q -> p j q", j=PACK)
+        u_raw = []
+        for qt in range(NQ // P):
+            raw = held.tile([P, PACK, P], F32, name="u_raw%d" % qt, align_bytes=64)
+            nc.sync.dma_start(out=raw[:], in_=u_rows[:, :, qt * P : (qt + 1) * P])
+            u_raw.append(raw)
 
-        v_grouped = held.tile([P, NQ, PACK], BF16, name="v_grouped", align_bytes=64)
-        quantised = {"v": quantise("v", v_raw, v_grouped)}
+        listed = held.tile([P, SLOTS], U8, name="listed", align_bytes=64)
+        planes = held.tile([P, SLOTS // 4], I32, name="planes", align_bytes=64)
+        nc.vector.tensor_copy(listed[:], k_scale_pool[:, 0 : TOKENS // 4].bitcast(U8).indirect(token_list[:]))
+        for quad in range(4):
+            first = SCALE_PARTITION + 4 * quad
+            nc.sync.dma_start(out=planes[32 * quad : 32 * quad + 4, :], in_=listed[:].bitcast(I32)[first : first + 4, :])
+        k_bytes = planes[:].bitcast(U8)
+
+        kb_row = shared.tile([P, SLOTS], F32, name="kb_row", align_bytes=64, offset=14592)
+        nc.scalar.activation(out=kb_row[:], in_=kb_pool[:].indirect(token_list[:]), func=ACT.Copy)
         turned = psum.tile([P, SLOTS // P, P], F32, name="turned")
         for blk in range(SLOTS // P):
             nc.tensor.transpose(turned[:, blk, :], kb_row[:, blk * P : (blk + 1) * P], identity[:])
-        kb_column = held.tile([P, SLOTS // P], F32, name="kb_column", align_bytes=64)
-        nc.scalar.copy(out=kb_column[:], in_=turned[:, :, KB_PARTITION])
-        c_codes = shared.tile([P, SLOTS], U32, name="c_codes", align_bytes=64, offset=0)
-        for half in range(2):
-            entries = distance_list[:, half * (HALF // 16) : (half + 1) * (HALF // 16)]
-            nc.vector.tensor_copy(
-                c_codes[:, half * HALF : (half + 1) * HALF], c_word_pool[:].bitcast(U32).indirect(entries)
+
+        def interleave(grouped, raw):
+            nc.scalar.copy(
+                out=grouped.rearrange("p (c i) j -> p c j i", i=4),
+                in_=raw.rearrange("p j (c i) -> p c j i", i=4),
             )
-        u_grouped = shared.tile([P, NQ, PACK], BF16, name="u_grouped", align_bytes=64, offset=2048)
-        quantised["u"] = quantise("u", u_raw, u_grouped)
+
+        def quantise(codes, scale_bytes, grouped):
+            nc.vector.quantize_mx(out=codes.bitcast(FP8X4), scales=scale_bytes, in_=grouped.rearrange("p q j -> p (q j)"))
+
+        c_codes = held.tile([P, SLOTS], U32, name="c_codes", align_bytes=64)
+        nc.vector.tensor_copy(c_codes[:], c_word_pool[:].bitcast(U32).indirect(distance_list[:]))
+        c_bytes = held.tile([P, SLOTS], U8, name="c_bytes", align_bytes=64)
+        nc.vector.tensor_copy(c_bytes[:], c_scale_pool[:, 0 : DISTANCES // 4].bitcast(U8).indirect(distance_list[:]))
+
+        v_first = shared.tile([P, P, PACK], BF16, name="v_first", align_bytes=64, offset=8448)
+        interleave(v_first[:], v_raw[:, :, 0:P])
+        kb_column = shared.tile([P, SLOTS // P], F32, name="kb_column", align_bytes=64, offset=16640)
+        nc.scalar.copy(out=kb_column[:], in_=turned[:, :, KB_PARTITION])
+        v_second = shared.tile([P, P, PACK], BF16, name="v_second", align_bytes=64, offset=14592)
+        interleave(v_second[:], v_raw[:, :, P:NQ])
         bias = held.tile([P, SLOTS], F32, name="bias", align_bytes=64)
         spread = psum.tile([P, SLOTS], F32, name="spread")
         for blk in range(SLOTS // P):
@@ -125,20 +115,22 @@ def tile_attend_txlsig_topk_kernel(tc, uT, vT, k_words, k_scales, c_words, c_sca
                 spread[:, blk * P : (blk + 1) * P], kb_column[:, blk : blk + 1].to_broadcast([P, P]), identity[:]
             )
         nc.scalar.copy(out=bias[:], in_=spread[:])
+        v_codes = held.tile([P, NQ], U32, name="v_codes", align_bytes=64)
+        v_bytes = shared.tile([P, NQ], U8, name="v_bytes", align_bytes=64, offset=16640)
+        quantise(v_codes[:, 0:P], v_bytes[:, 0:P], v_first[:])
+        quantise(v_codes[:, P:NQ], v_bytes[:, P:NQ], v_second[:])
 
-        pieces = [(half, qt) for half in range(2) for qt in range(NQ // P)]
+        pieces = [(qt, half) for qt in range(NQ // P) for half in range(2)]
         acc = {}
         for piece in pieces:
             acc[piece] = psum.tile([P, HALF], F32, name="acc%d_%d" % piece)
 
-        def product(piece, queries, codes, scale_bytes, first_pass):
-            half, qt = piece
-            q_cols = slice(qt * P, (qt + 1) * P)
-            s_cols = slice(half * HALF, (half + 1) * HALF)
+        def product(piece, q_codes, q_bytes, codes, scale_bytes, first_pass):
+            s_cols = slice(piece[1] * HALF, (piece[1] + 1) * HALF)
             nc.tensor.matmul_mx(
                 out=acc[piece][:],
-                lhsT=quantised[queries][0][:, q_cols].bitcast(FP8X4),
-                lhsT_scale=quantised[queries][1][:, q_cols],
+                lhsT=q_codes.bitcast(FP8X4),
+                lhsT_scale=q_bytes,
                 rhs=codes[:, s_cols].bitcast(FP8X4),
                 rhs_scale=scale_bytes[:, s_cols],
                 start=first_pass,
@@ -146,18 +138,28 @@ def tile_attend_txlsig_topk_kernel(tc, uT, vT, k_words, k_scales, c_words, c_sca
             )
 
         for piece in pieces:
-            product(piece, "v", c_codes, c_bytes, True)
+            q_cols = slice(piece[0] * P, (piece[0] + 1) * P)
+            product(piece, v_codes[:, q_cols], v_bytes[:, q_cols], c_codes, c_bytes, True)
 
-        k_codes = held.tile([P, SLOTS], U32, name="k_codes", tag="k_codes", align_bytes=64)
+        k_codes = shared.tile([P, SLOTS], U32, name="k_codes", align_bytes=64, offset=9408)
         for half in range(2):
             entries = token_list[:, half * (HALF // 16) : (half + 1) * (HALF // 16)]
             nc.vector.tensor_copy(
                 k_codes[:, half * HALF : (half + 1) * HALF], k_word_pool[:].bitcast(U32).indirect(entries)
             )
 
+        u_quantised = []
+        for qt in range(NQ // P):
+            grouped = shared.tile([P, P, PACK], BF16, name="u_grouped%d" % qt, align_bytes=64, offset=(7488, 14592)[qt])
+            interleave(grouped[:], u_raw[qt][:])
+            u_codes = held.tile([P, P], U32, name="u_codes%d" % qt, align_bytes=64)
+            u_bytes = held.tile([P, P], U8, name="u_bytes%d" % qt, align_bytes=64)
+            quantise(u_codes[:], u_bytes[:], grouped[:])
+            u_quantised.append((u_codes, u_bytes))
+
         for piece in pieces:
-            half, qt = piece
-            product(piece, "u", k_codes, k_bytes, False)
+            qt, half = piece
+            product(piece, u_quantised[qt][0][:], u_quantised[qt][1][:], k_codes, k_bytes, False)
             width = LAST_WIDTH if piece == pieces[-1] else HALF
             for col in range(0, HALF, width):
                 s_cols = slice(half * HALF + col, half * HALF + col + width)

@@ -23,7 +23,7 @@ TOKENS = 2048
 DISTANCES = 1024
 KB_PARTITION = 127
 SCALE_PARTITION = 112
-LAST_WIDTH = 128
+FIRST_WIDTH = 128
 
 FLOPS = 2 * 2 * D * NQ * SLOTS
 BYTES = 3219456
@@ -102,12 +102,10 @@ def tile_attend_txlsig_topk_kernel(tc, uT, vT, k_words, k_scales, c_words, c_sca
         c_bytes = held.tile([P, SLOTS], U8, name="c_bytes", align_bytes=64)
         nc.vector.tensor_copy(c_bytes[:], c_scale_pool[:, 0 : DISTANCES // 4].bitcast(U8).indirect(distance_list[:]))
 
-        v_first = shared.tile([P, P, PACK], BF16, name="v_first", align_bytes=64, offset=8448)
-        interleave(v_first[:], v_raw[:, :, 0:P])
-        kb_column = shared.tile([P, SLOTS // P], F32, name="kb_column", align_bytes=64, offset=16640)
+        kb_column = shared.tile([P, SLOTS // P], F32, name="kb_column", align_bytes=64, offset=16704)
         nc.scalar.copy(out=kb_column[:], in_=turned[:, :, KB_PARTITION])
-        v_second = shared.tile([P, P, PACK], BF16, name="v_second", align_bytes=64, offset=14592)
-        interleave(v_second[:], v_raw[:, :, P:NQ])
+        v_grouped = shared.tile([P, NQ, PACK], BF16, name="v_grouped", align_bytes=64, offset=14592)
+        interleave(v_grouped[:], v_raw[:])
         bias = held.tile([P, SLOTS], F32, name="bias", align_bytes=64)
         spread = psum.tile([P, SLOTS], F32, name="spread")
         for blk in range(SLOTS // P):
@@ -116,9 +114,8 @@ def tile_attend_txlsig_topk_kernel(tc, uT, vT, k_words, k_scales, c_words, c_sca
             )
         nc.scalar.copy(out=bias[:], in_=spread[:])
         v_codes = held.tile([P, NQ], U32, name="v_codes", align_bytes=64)
-        v_bytes = shared.tile([P, NQ], U8, name="v_bytes", align_bytes=64, offset=16640)
-        quantise(v_codes[:, 0:P], v_bytes[:, 0:P], v_first[:])
-        quantise(v_codes[:, P:NQ], v_bytes[:, P:NQ], v_second[:])
+        v_bytes = shared.tile([P, NQ], U8, name="v_bytes", align_bytes=64, offset=16704)
+        quantise(v_codes[:], v_bytes[:], v_grouped[:])
 
         pieces = [(qt, half) for qt in range(NQ // P) for half in range(2)]
         acc = {}
@@ -141,16 +138,12 @@ def tile_attend_txlsig_topk_kernel(tc, uT, vT, k_words, k_scales, c_words, c_sca
             q_cols = slice(piece[0] * P, (piece[0] + 1) * P)
             product(piece, v_codes[:, q_cols], v_bytes[:, q_cols], c_codes, c_bytes, True)
 
-        k_codes = shared.tile([P, SLOTS], U32, name="k_codes", align_bytes=64, offset=9408)
-        for half in range(2):
-            entries = token_list[:, half * (HALF // 16) : (half + 1) * (HALF // 16)]
-            nc.vector.tensor_copy(
-                k_codes[:, half * HALF : (half + 1) * HALF], k_word_pool[:].bitcast(U32).indirect(entries)
-            )
+        k_codes = shared.tile([P, SLOTS], U32, name="k_codes", align_bytes=64, offset=12608)
+        nc.vector.tensor_copy(k_codes[:], k_word_pool[:].bitcast(U32).indirect(token_list[:]))
 
         u_quantised = []
         for qt in range(NQ // P):
-            grouped = shared.tile([P, P, PACK], BF16, name="u_grouped%d" % qt, align_bytes=64, offset=(7488, 14592)[qt])
+            grouped = shared.tile([P, P, PACK], BF16, name="u_grouped%d" % qt, align_bytes=64, offset=(14656, 15680)[qt])
             interleave(grouped[:], u_raw[qt][:])
             u_codes = held.tile([P, P], U32, name="u_codes%d" % qt, align_bytes=64)
             u_bytes = held.tile([P, P], U8, name="u_bytes%d" % qt, align_bytes=64)
@@ -160,7 +153,7 @@ def tile_attend_txlsig_topk_kernel(tc, uT, vT, k_words, k_scales, c_words, c_sca
         for piece in pieces:
             qt, half = piece
             product(piece, u_quantised[qt][0][:], u_quantised[qt][1][:], k_codes, k_bytes, False)
-            width = LAST_WIDTH if piece == pieces[-1] else HALF
+            width = FIRST_WIDTH if piece == pieces[0] else HALF
             for col in range(0, HALF, width):
                 s_cols = slice(half * HALF + col, half * HALF + col + width)
                 label = "%d_%d_%d" % (qt, half, col)

@@ -23,7 +23,6 @@ TOKENS = 2048
 DISTANCES = 1024
 KB_PARTITION = 127
 SCALE_PARTITION = 112
-FIRST_WIDTH = 128
 
 FLOPS = 2 * 2 * D * NQ * SLOTS
 BYTES = 3219456
@@ -117,15 +116,15 @@ def tile_attend_txlsig_topk_kernel(tc, uT, vT, k_words, k_scales, c_words, c_sca
         v_bytes = shared.tile([P, NQ], U8, name="v_bytes", align_bytes=64, offset=16704)
         quantise(v_codes[:], v_bytes[:], v_grouped[:])
 
-        pieces = [(qt, half) for qt in range(NQ // P) for half in range(2)]
+        banks = [(0, 0, P), (0, P, P), (0, HALF, HALF), (1, 0, HALF), (1, HALF, HALF)]
         acc = {}
-        for piece in pieces:
-            acc[piece] = psum.tile([P, HALF], F32, name="acc%d_%d" % piece)
+        for bank in banks:
+            acc[bank] = psum.tile([P, bank[2]], F32, name="acc%d_%d" % bank[:2])
 
-        def product(piece, q_codes, q_bytes, codes, scale_bytes, first_pass):
-            s_cols = slice(piece[1] * HALF, (piece[1] + 1) * HALF)
+        def product(bank, q_codes, q_bytes, codes, scale_bytes, first_pass):
+            s_cols = slice(bank[1], bank[1] + bank[2])
             nc.tensor.matmul_mx(
-                out=acc[piece][:],
+                out=acc[bank][:],
                 lhsT=q_codes.bitcast(FP8X4),
                 lhsT_scale=q_bytes,
                 rhs=codes[:, s_cols].bitcast(FP8X4),
@@ -134,9 +133,9 @@ def tile_attend_txlsig_topk_kernel(tc, uT, vT, k_words, k_scales, c_words, c_sca
                 stop=not first_pass,
             )
 
-        for piece in pieces:
-            q_cols = slice(piece[0] * P, (piece[0] + 1) * P)
-            product(piece, v_codes[:, q_cols], v_bytes[:, q_cols], c_codes, c_bytes, True)
+        for bank in banks:
+            q_cols = slice(bank[0] * P, (bank[0] + 1) * P)
+            product(bank, v_codes[:, q_cols], v_bytes[:, q_cols], c_codes, c_bytes, True)
 
         k_codes = shared.tile([P, SLOTS], U32, name="k_codes", align_bytes=64, offset=12608)
         nc.vector.tensor_copy(k_codes[:], k_word_pool[:].bitcast(U32).indirect(token_list[:]))
@@ -150,22 +149,22 @@ def tile_attend_txlsig_topk_kernel(tc, uT, vT, k_words, k_scales, c_words, c_sca
             quantise(u_codes[:], u_bytes[:], grouped[:])
             u_quantised.append((u_codes, u_bytes))
 
-        for piece in pieces:
-            qt, half = piece
-            product(piece, u_quantised[qt][0][:], u_quantised[qt][1][:], k_codes, k_bytes, False)
-            width = FIRST_WIDTH if piece == pieces[0] else HALF
-            for col in range(0, HALF, width):
-                s_cols = slice(half * HALF + col, half * HALF + col + width)
-                label = "%d_%d_%d" % (qt, half, col)
-                logit = held.tile([P, width], F32, name="logit" + label, align_bytes=64)
+        for bank in banks:
+            qt, first, width = bank
+            product(bank, u_quantised[qt][0][:], u_quantised[qt][1][:], k_codes, k_bytes, False)
+            step = width
+            for col in range(0, width, step):
+                s_cols = slice(first + col, first + col + step)
+                label = "%d_%d" % (qt, first + col)
+                logit = held.tile([P, step], F32, name="logit" + label, align_bytes=64)
                 nc.vector.scalar_tensor_tensor(
                     out=logit[:],
-                    in0=acc[piece][:, col : col + width],
+                    in0=acc[bank][:, col : col + step],
                     scalar=0.25,
                     in1=bias[:, s_cols],
                     op0=ALU.mult,
                     op1=ALU.add,
                 )
-                weight = held.tile([P, width], F32, name="weight" + label, align_bytes=64)
+                weight = held.tile([P, step], F32, name="weight" + label, align_bytes=64)
                 nc.scalar.activation(out=weight[:], in_=logit[:], func=ACT.Sigmoid)
                 nc.sync.dma_start(out=out[0, qt * P : (qt + 1) * P, s_cols], in_=weight[:])

@@ -50,8 +50,9 @@ def tile_attend_txlsig_topk_kernel(tc, uT, vT, k_words, k_scales, c_words, c_sca
         nc.gpsimd.memset(warm_in[:], 0.0)
         nc.vector.memset(c_scale_pool[:], 0)
         nc.vector.memset(k_scale_pool[0:SCALE_PARTITION, :], 0)
-        nc.gpsimd.memset(kb_pool[0:KB_PARTITION, :], 0.0)
         make_identity(nc, identity[:])
+        nc.gpsimd.memset(kb_pool[0:KB_PARTITION, 0 : TOKENS // 2], 0.0)
+        nc.vector.memset(kb_pool[0:KB_PARTITION, TOKENS // 2 : TOKENS], 0.0)
 
         nc.sync.dma_start(token_list[:], offs)
         nc.scalar.dma_start(out=kb_pool[KB_PARTITION:P, :], in_=kb[0:1, :])

from contextlib import ExitStack

import concourse.mybir as mybir
from concourse.masks import make_identity

F32 = mybir.dt.float32
BF16 = mybir.dt.bfloat16
I32 = mybir.dt.int32
U32 = mybir.dt.uint32
U16 = mybir.dt.uint16
U8 = mybir.dt.uint8
FP8X4 = mybir.dt.float8_e4m3fn_x4
ACT = mybir.ActivationFunctionType
ALU = mybir.AluOpType

P = 128
PACK = 4
D = 512
NQ = 256
SLOTS = 512
HALF = 256
TOKENS = 2048
DISTANCES = 1024
KB_PARTITION = 127
SCALE_PARTITION = 112

FLOPS = 2 * 2 * D * NQ * SLOTS
BYTES = 3219456


def tile_attend_txlsig_topk_kernel(tc, uT, vT, k_words, k_scales, c_words, c_scales, kb, offs, offs2, out):
    nc = tc.nc
    with ExitStack() as ctx:
        held = ctx.enter_context(tc.tile_pool(name="held", bufs=1))
        shared = ctx.enter_context(tc.tile_pool(name="shared", bufs=1))
        psum = ctx.enter_context(tc.psum_pool(name="psum", bufs=1))

        token_list = held.tile([P, SLOTS // 16], U16, name="token_list")
        distance_list = held.tile([P, SLOTS // 16], U16, name="distance_list")
        k_word_pool = held.tile([P, TOKENS], I32, name="k_word_pool", align_bytes=64)
        c_word_pool = held.tile([P, DISTANCES], I32, name="c_word_pool", align_bytes=64)
        k_scale_pool = held.tile([P, TOKENS // 4 + 1], I32, name="k_scale_pool", align_bytes=64)
        c_scale_pool = held.tile([P, DISTANCES // 4 + 1], I32, name="c_scale_pool", align_bytes=64)
        kb_pool = shared.tile([P, TOKENS], F32, name="kb_pool", align_bytes=64, offset=6400)
        v_raw = held.tile([P, PACK, NQ], F32, name="v_raw", align_bytes=64)
        identity = held.tile([P, P], F32, name="identity", align_bytes=64)

        warm_in = held.tile([P, 1], F32, name="warm_in", align_bytes=64)
        warm_out = held.tile([P, 1], F32, name="warm_out", align_bytes=64)
        nc.gpsimd.memset(warm_in[:], 0.0)
        nc.vector.memset(c_scale_pool[:], 0)
        nc.vector.memset(k_scale_pool[0:SCALE_PARTITION, :], 0)
        make_identity(nc, identity[:])
        nc.gpsimd.memset(kb_pool[0:KB_PARTITION, 0 : TOKENS // 2], 0.0)
        nc.vector.memset(kb_pool[0:KB_PARTITION, TOKENS // 2 : TOKENS], 0.0)

        nc.sync.dma_start(token_list[:], offs)
        nc.scalar.dma_start(out=kb_pool[KB_PARTITION:P, :], in_=kb[0:1, :])
        nc.sync.dma_start(out=k_scale_pool[SCALE_PARTITION:P, 0 : TOKENS // 4], in_=k_scales[0].bitcast(I32))
        nc.sync.dma_start(out=c_word_pool[:], in_=c_words[0].rearrange("p n t -> p (n t)").bitcast(I32))
        nc.scalar.activation(out=warm_out[:], in_=warm_in[:], func=ACT.Sigmoid)
        nc.sync.dma_start(distance_list[:], offs2)
        nc.sync.dma_start(out=v_raw[:], in_=vT[0].rearrange("(p j) q -> p j q", j=PACK))
        for row in range(4):
            nc.sync.dma_start(
                out=c_scale_pool[row:P:32, 0 : DISTANCES // 4], in_=c_scales[0].bitcast(I32)[row:16:4, :]
            )
        nc.sync.dma_start(out=k_word_pool[:], in_=k_words[0].rearrange("p n t -> p (n t)").bitcast(I32))

        u_rows = uT[0].rearrange("(p j) q -> p j q", j=PACK)
        u_raw = []
        for qt in range(NQ // P):
            raw = held.tile([P, PACK, P], F32, name="u_raw%d" % qt, align_bytes=64)
            nc.sync.dma_start(out=raw[:], in_=u_rows[:, :, qt * P : (qt + 1) * P])
            u_raw.append(raw)

        listed = held.tile([P, SLOTS], U8, name="listed", align_bytes=64)
        planes = held.tile([P, SLOTS // 4], I32, name="planes", align_bytes=64)
        nc.vector.tensor_copy(listed[:], k_scale_pool[:, 0 : TOKENS // 4].bitcast(U8).indirect(token_list[:]))
        for quad in range(4):
            first = SCALE_PARTITION + 4 * quad
            nc.sync.dma_start(out=planes[32 * quad : 32 * quad + 4, :], in_=listed[:].bitcast(I32)[first : first + 4, :])
        k_bytes = planes[:].bitcast(U8)

        kb_row = shared.tile([P, SLOTS], F32, name="kb_row", align_bytes=64, offset=14592)
        nc.scalar.activation(out=kb_row[:], in_=kb_pool[:].indirect(token_list[:]), func=ACT.Copy)
        turned = psum.tile([P, SLOTS // P, P], F32, name="turned")
        for blk in range(SLOTS // P):
            nc.tensor.transpose(turned[:, blk, :], kb_row[:, blk * P : (blk + 1) * P], identity[:])

        def interleave(grouped, raw):
            nc.scalar.copy(
                out=grouped.rearrange("p (c i) j -> p c j i", i=4),
                in_=raw.rearrange("p j (c i) -> p c j i", i=4),
            )

        def quantise(codes, scale_bytes, grouped):
            nc.vector.quantize_mx(out=codes.bitcast(FP8X4), scales=scale_bytes, in_=grouped.rearrange("p q j -> p (q j)"))

        c_codes = held.tile([P, SLOTS], U32, name="c_codes", align_bytes=64)
        nc.vector.tensor_copy(c_codes[:], c_word_pool[:].bitcast(U32).indirect(distance_list[:]))
        c_bytes = held.tile([P, SLOTS], U8, name="c_bytes", align_bytes=64)
        nc.vector.tensor_copy(c_bytes[:], c_scale_pool[:, 0 : DISTANCES // 4].bitcast(U8).indirect(distance_list[:]))

        kb_column = shared.tile([P, SLOTS // P], F32, name="kb_column", align_bytes=64, offset=16704)
        nc.scalar.copy(out=kb_column[:], in_=turned[:, :, KB_PARTITION])
        v_grouped = shared.tile([P, NQ, PACK], BF16, name="v_grouped", align_bytes=64, offset=14592)
        interleave(v_grouped[:], v_raw[:])
        bias = held.tile([P, SLOTS], F32, name="bias", align_bytes=64)
        spread = psum.tile([P, SLOTS], F32, name="spread")
        for blk in range(SLOTS // P):
            nc.tensor.transpose(
                spread[:, blk * P : (blk + 1) * P], kb_column[:, blk : blk + 1].to_broadcast([P, P]), identity[:]
            )
        nc.scalar.copy(out=bias[:], in_=spread[:])
        v_codes = held.tile([P, NQ], U32, name="v_codes", align_bytes=64)
        v_bytes = shared.tile([P, NQ], U8, name="v_bytes", align_bytes=64, offset=16704)
        quantise(v_codes[:], v_bytes[:], v_grouped[:])

        banks = [(0, 0, P), (0, P, P), (0, HALF, HALF), (1, 0, HALF), (1, HALF, HALF)]
        acc = {}
        for bank in banks:
            acc[bank] = psum.tile([P, bank[2]], F32, name="acc%d_%d" % bank[:2])

        def product(bank, q_codes, q_bytes, codes, scale_bytes, first_pass):
            s_cols = slice(bank[1], bank[1] + bank[2])
            nc.tensor.matmul_mx(
                out=acc[bank][:],
                lhsT=q_codes.bitcast(FP8X4),
                lhsT_scale=q_bytes,
                rhs=codes[:, s_cols].bitcast(FP8X4),
                rhs_scale=scale_bytes[:, s_cols],
                start=first_pass,
                stop=not first_pass,
            )

        for bank in banks:
            q_cols = slice(bank[0] * P, (bank[0] + 1) * P)
            product(bank, v_codes[:, q_cols], v_bytes[:, q_cols], c_codes, c_bytes, True)

        k_codes = shared.tile([P, SLOTS], U32, name="k_codes", align_bytes=64, offset=12608)
        nc.vector.tensor_copy(k_codes[:], k_word_pool[:].bitcast(U32).indirect(token_list[:]))

        u_quantised = []
        for qt in range(NQ // P):
            grouped = shared.tile([P, P, PACK], BF16, name="u_grouped%d" % qt, align_bytes=64, offset=(14656, 15680)[qt])
            interleave(grouped[:], u_raw[qt][:])
            u_codes = held.tile([P, P], U32, name="u_codes%d" % qt, align_bytes=64)
            u_bytes = held.tile([P, P], U8, name="u_bytes%d" % qt, align_bytes=64)
            quantise(u_codes[:], u_bytes[:], grouped[:])
            u_quantised.append((u_codes, u_bytes))

        for bank in banks:
            qt, first, width = bank
            product(bank, u_quantised[qt][0][:], u_quantised[qt][1][:], k_codes, k_bytes, False)
            step = width
            for col in range(0, width, step):
                s_cols = slice(first + col, first + col + step)
                label = "%d_%d" % (qt, first + col)
                logit = held.tile([P, step], F32, name="logit" + label, align_bytes=64)
                nc.vector.scalar_tensor_tensor(
                    out=logit[:],
                    in0=acc[bank][:, col : col + step],
                    scalar=0.25,
                    in1=bias[:, s_cols],
                    op0=ALU.mult,
                    op1=ALU.add,
                )
                weight = held.tile([P, step], F32, name="weight" + label, align_bytes=64)
                nc.scalar.activation(out=weight[:], in_=logit[:], func=ACT.Sigmoid)
                nc.sync.dma_start(out=out[0, qt * P : (qt + 1) * P, s_cols], in_=weight[:])
